import numpy as np, ml_dtypes
CORES = [5,29,101,125,133,157,229,253]
N = 8
BF = ml_dtypes.bfloat16
V, M, T = 256, 1, 5
WIN = N * V
HI = WIN // 16
B = V // M
H = (N, 8, 16, V)
def sized(u, hi):
    return np.where(u < 0, -1.0, 1.0) * np.clip(np.abs(u), 0.125, hi)
def draw(rng):
    return {"x": np.minimum((rng.random(H) * rng.choice(np.array([8, 16, 16, 24]), (N, 8, 1, V))).astype(np.int64), 15),
            "u": sized(rng.standard_normal(H, dtype=np.float32) * np.exp2(rng.integers(-1, 1, (N, 8, 16, 1))), 3.0),
            "w": (rng.random(H) * rng.choice(np.array([4, 8, 12, 16]), (N, 8, 1, V))).astype(np.int64),
            "ag": rng.choice(np.array([0, 1, 2, 3, 3, 3]), H), "s": rng.integers(0, WIN, H), "p": rng.integers(0, WIN, H),
            "j": rng.integers(0, HI, (N, 8, 16, WIN)), "tb": rng.integers(30, 110, (N, 8, 16)), "te": rng.integers(40, 200, (N, 8, 16))}
def pack(d):
    o = {}
    o["x0"] = d["x"].reshape(N, 128, V).astype(np.float32).astype(BF)
    o["u0"] = d["u"].reshape(N, 128, V).astype(np.float32)
    o["s0"] = d["s"].reshape(N, 128, V).astype(np.int32)
    o["p0"] = d["p"].reshape(N, 128, V).astype(np.int32)
    o["w0"] = d["w"].reshape(N, 128, V).astype(np.float32).astype(BF)
    o["ag"] = d["ag"].reshape(N, 128, V).astype(np.float32).astype(BF)
    o["ax"] = d["j"].reshape(N, 128, WIN).astype(np.float32).astype(BF)
    o["th"] = np.stack([d["tb"], d["te"]], axis=-1).reshape(N, 128, 2).astype(np.int32)
    return o
def ends(rng, lo, hi, shape, share):
    e = np.where(rng.random(shape) < 0.5, lo, hi)
    return np.where(rng.random(shape) < share, e, rng.integers(lo, hi + 1, shape))
def setup_inputs(rng):
    return pack(draw(rng))
def setup_inputs_spread(rng):
    d = draw(rng); c = (N, 8, 1, V)
    d["u"] = sized(d["u"] * np.exp2(rng.integers(-1, 2, c)), 8.0)
    d["x"] = np.minimum((np.exp2(4 * rng.random(H)) - 1).astype(np.int64) + rng.integers(0, 4, c), 15)
    d["w"] = np.minimum(np.exp2(4 * rng.random(H)).astype(np.int64), 15) * (rng.random(H) > 0.1)
    d["tb"] = rng.integers(0, 241, (N, 8, 16)); d["te"] = rng.integers(0, 241, (N, 8, 16))
    return pack(d)
def setup_inputs_ends(rng):
    d = draw(rng)
    d["x"] = ends(rng, 0, 15, H, 1.0)
    d["w"] = 15 * (rng.random(H) < rng.choice(np.array([0.0, 0.1, 0.2, 1.0]), (N, 8, 1, V))).astype(np.int64)
    d["ag"] = ends(rng, 0, 3, H, 0.8)
    d["s"] = ends(rng, 0, WIN - 1, H, 0.7); d["p"] = ends(rng, 0, WIN - 1, H, 0.7)
    d["j"] = ends(rng, 0, HI - 1, (N, 8, 16, WIN), 0.7)
    d["tb"] = ends(rng, 0, 240, (N, 8, 16), 0.8); d["te"] = ends(rng, 0, 240, (N, 8, 16), 0.8)
    d["u"] = np.where(rng.random(H) < 0.5, -1.0, 1.0) * np.where(rng.random(H) < 0.5, 0.125, 8.0)
    d["u"][:, ::2, :, V - 2:] = 8.0; d["u"][:, 1::2, :, V - 2:] = -8.0
    low = np.where(rng.permutation(8) < 4, 0, 15)[:, None, None]
    d["x"][0, :, :, :16] = low; d["w"][0, :, :, :16] = low
    d["x"][N - 1, :, :, V - 32:] = 15; d["w"][N - 1, :, :, V - 32:] = 15
    d["x"][:, :, :, V - 2:] = 15; d["w"][:, :, :, V - 2:] = 15
    d["ag"][:, :, :, V - 1] = 0; d["p"][:, :, :, V - 1] = WIN - 1
    d["ag"][:, :, :, V - 2] = 3; d["s"][:, :, :, V - 2] = WIN - 1
    d["x"][:, :, :, V - 3] = 0; d["w"][:, :, :, V - 3] = 0; d["ag"][:, :, :, V - 3] = 0
    d["te"][:, 7, 15] = 240; d["te"][:, 7, 0] = 0; d["tb"][:, 7, 15] = 240; d["tb"][:, 7, 0] = 0
    return pack(d)
def setup_inputs_corners(rng):
    d = draw(rng)
    lev = np.broadcast_to(rng.choice(np.array([0, 3, 6, 11, 15]), (N, 8, 1, V)), H)
    d["x"][:, ::2] = lev[:, ::2]
    many = rng.choice(np.array([0, 1, 2, 3, 4, 5, 6, 7, 8, 9, 15, 16]), (N, 8, 1, V))
    many[:, 3] = 16; many[::2, 4] = 0
    live = np.argsort(rng.random(H), axis=2) < many
    age = rng.integers(0, 3, H); age[:, 0] = 2; age[:, 1] = 0; age[:, 2] = 1
    d["ag"] = np.where(live, age, 3)
    d["w"] = rng.choice(np.array([0, 0, 0, 1, 1, 4, 11, 12, 15]), H)
    own = np.arange(N)[:, None, None, None] * V + np.arange(V)
    for k in ("s", "p"):
        c = rng.integers(0, 6, H)
        d[k] = np.where(c == 0, own, np.where(c == 1, 0, np.where(c == 2, WIN - 1, d[k])))
    for q in range(N):
        m = (8, 4, 0, 7, 1, 6, 3, 2)[q]
        d["te"][q] = np.where(rng.permutation(8) < m, 0, 240)[:, None]
    d["tb"] = rng.choice(np.array([0, 1, 60, 100, 239, 240]), (N, 8, 16))
    return pack(d)
def setup_inputs_crowd(rng):
    d = draw(rng); o = rng.permutation(8); z = rng.integers(0, WIN, 8); h = (N, 16, V)
    for i in range(4):
        g = int(o[i]); q = int(z[g]) // V; v = int(z[g]) % V
        d["s"][:, g] = z[g]; d["p"][:, g] = z[g]; d["ag"][:, g] = rng.integers(0, 3, h)
        d["x"][q, g, :, v] = rng.integers(4, 16, 16); d["w"][q, g, :, v] = 8
        if i >= 2:
            one = np.arange(16)[:, None] == rng.integers(0, 16, (N, 1, V))
            d["p"][:, g] = np.where(one, rng.integers(0, WIN, h), z[g]); d["s"][:, g] = np.where(one, rng.integers(0, WIN, h), z[g])
    g = int(o[4]); few = rng.integers(0, WIN, 4)
    d["s"][:, g] = rng.choice(few, h); d["p"][:, g] = rng.choice(few, h)
    keep = d["te"][1].copy(); d["te"][:] = 0; d["te"][:, int(o[7]), 1::2] = 240; d["te"][1] = keep
    return pack(d)
def setup_inputs_calm(rng):
    d = draw(rng); turn = int(rng.integers(0, 4))
    for q in range(N):
        d["te"][q] = np.where(rng.permutation(8) < q % 4, 0, 240)[:, None]
    d["ag"] = np.broadcast_to(((np.arange(8) + turn) % 4)[None, :, None, None], H).copy()
    lev = np.broadcast_to(rng.choice(np.array([3, 6, 9, 12]), (N, 8, 1, V)), H)
    d["x"][:, 1::2] = lev[:, 1::2]
    d["tb"] = rng.choice(np.array([0, 40, 80]), (N, 8, 16))
    return pack(d)
def check_ranges(d):
    bad = []
    for k, lo, hi in (("x0", 0, 15), ("s0", 0, WIN - 1), ("p0", 0, WIN - 1), ("w0", 0, 15), ("ag", 0, 3), ("ax", 0, HI - 1), ("th", 0, 240), ("u0", -8, 8)):
        v = np.asarray(d[k]).astype(np.float64)
        if not (np.min(v) >= lo and np.max(v) <= hi): bad.append("range of " + k)
        if k != "u0" and np.any(v != np.floor(v)): bad.append("whole numbers of " + k)
        if k == "u0" and not np.min(np.abs(v)) >= 0.125: bad.append("least size of " + k)
    return bad
def reference(x0, u0, s0, p0, w0, ag, ax, th):
    X, W, A = [a.astype(np.float32).astype(np.int64).reshape(H) for a in (x0, w0, ag)]
    S, P = [a.astype(np.int64).reshape(H) for a in (s0, p0)]
    U = u0.astype(np.float64).reshape(H); J = ax.astype(np.float32).astype(np.int64).reshape(N, 8, 16, WIN)
    tb = th[:, :, 0].astype(np.int64).reshape(N, 8, 16, 1); te = th[:, :, 1].astype(np.int64).reshape(N, 8, 16, 1)
    gi = np.arange(8)[:, None, None, None]; ii = np.arange(16)[None, :, None, None]; K = np.arange(16)[:, None]
    for t in range(T):
        a = (t % M) * B; b = a + B
        XA = X.transpose(1, 2, 0, 3).reshape(8, 16, WIN); UA = U.transpose(1, 2, 0, 3).reshape(8, 16, WIN)
        s = S[..., a:b]; p = P[..., a:b]; e = W[..., a:b]; age = A[..., a:b]
        live = age < 3
        C = np.where(live, p, s)
        w = e * (4 - np.where(live, age, 0))
        c = np.zeros((N, 8, 16, B), np.int64); sx = np.zeros((N, 8, 16, B), np.int64); su = np.zeros((N, 8, 16, B))
        for r in range(N):
            ix = C[r][:, None]; wr = w[r][:, None]
            XC = XA[gi, ii, ix]
            c[r] = np.sum(np.minimum(XC, X[r][:, :, None, a:b]), axis=1)
            sx[r] = np.sum(wr * XC, axis=2)
            su[r] = np.sum(wr * UA[gi, ii, ix], axis=2)
        nx = np.minimum(sx >> 8, 15)
        nu = np.tanh(su * 2.0 ** -11 + 0.5 * U[..., a:b] + 0.0625 * (X[..., a:b] - 8))
        strong = np.sum(nx, axis=2, keepdims=True) >= te
        n = np.sum(strong.astype(np.int64), axis=1, keepdims=True)
        key = np.where(live, 16 * c + 15 - K, -1)
        before = np.sum((key[:, :, :, None] > key[:, :, None]).astype(np.int64), axis=2)
        cap = live & strong & (before < n)
        fresh = ~live & (c >= tb)
        q = (C + 16 * np.take_along_axis(J, C, 3) + K) & (WIN - 1)
        s2 = np.where(cap, p, s); e2 = np.where(cap, np.minimum(e + 4, 15), e); p2 = np.where(fresh, q, p)
        a2 = np.where(cap, 3, np.where(live, age + 1, np.where(fresh, 0, 3)))
        S[..., a:b] = s2; W[..., a:b] = e2; P[..., a:b] = p2; A[..., a:b] = a2; X[..., a:b] = nx; U[..., a:b] = nu
    Y = np.where(A < 3, P, S)
    return {"yx": X.reshape(N, 128, V).astype(np.float32), "yu": U.reshape(N, 128, V).astype(np.float32), "yc": Y.reshape(N, 128, V).astype(np.float32), "yw": (16 * A + W).reshape(N, 128, V).astype(np.float32)}

def check_inputs(d):
    bad = list(check_ranges(d))
    if not bad:
        for name, y in reference(**d).items():
            for q in range(N):
                v = np.abs(np.asarray(y[q], np.float64)); s = np.sqrt(np.mean(v * v))
                if v.max() > 6 * s or s < 2.0 ** -3: bad.append('%s of rank %d is uneven or too small' % (name, q))
    return bad

@@ -1,0 +1,621 @@
+from concourse.bass import DstId, RemoteDMATransfer
+from concourse.mybir import AluOpType, ActivationFunctionType
+
+ALU = AluOpType
+ACT = ActivationFunctionType
+STEPS, V, WIN = 5, 256, 2048
+
+SCRATCH = {
+    "tx0": ("sbuf", [128, WIN], "bfloat16"), "tx1": ("sbuf", [128, WIN], "bfloat16"),
+    "tu0": ("sbuf", [128, WIN], "float32"), "tu1": ("sbuf", [128, WIN], "float32"),
+    "jt": ("sbuf", [128, WIN], "bfloat16"),
+    "xc": ("sbuf", [128, 16 * V], "bfloat16"),
+    "ws0": ("sbuf", [128, 16 * V], "bfloat16"), "ws1": ("sbuf", [128, 16 * V], "bfloat16"),
+    "wx": ("sbuf", [128, 2048], "float16"),
+    "mn": ("sbuf", [128, 4096], "bfloat16"),
+    "wu": ("sbuf", [128, 2048], "float32"),
+    "jg": ("sbuf", [128, 2048], "bfloat16"),
+    "sg": ("sbuf", [128, 2048], "bfloat16"),
+    "selw": ("sbuf", [128, 2048], "bfloat16"), "jd": ("sbuf", [128, 2048], "bfloat16"),
+    "shm": ("sbuf", [128, 1024], "bfloat16"), "trm": ("sbuf", [128, 1024], "bfloat16"),
+    "cm": ("sbuf", [128, 128 * 15], "bfloat16"),
+    "gsel": ("sbuf", [128, 144], "bfloat16"), "gneg": ("sbuf", [128, 144], "bfloat16"),
+    "seg": ("sbuf", [128, 1024], "bfloat16"), "su": ("sbuf", [128, 1024], "float32"),
+    "ik": ("sbuf", [128, 128], "int32"),
+    "i16": ("sbuf", [128, 128], "float16"),
+    "i32": ("sbuf", [128, 256], "float32"),
+    "ia": ("sbuf", [128, 128], "int32"), "ib": ("sbuf", [128, 128], "int32"), "ic": ("sbuf", [128, 144], "int32"),
+    "ip": ("sbuf", [128, 16], "int32"),
+    "col": ("sbuf", [128, 48], "float32"),
+    "thi": ("sbuf", [128, 2], "int32"),
+    "si": ("sbuf", [128, V], "int32"), "ci": ("sbuf", [128, V], "int32"), "cr": ("sbuf", [128, V], "int32"),
+    "off": ("sbuf", [128, 3 * V], "uint16"),
+    "sb": ("sbuf", [128, 16 * V], "bfloat16"),
+    "sf": ("sbuf", [128, 6 * V], "float32"),
+    "pw0": ("psum", [128, 512], "float32"), "pw1": ("psum", [128, 512], "float32"),
+    "pw2": ("psum", [128, 512], "float32"), "ph": ("psum", [128, 512], "float32"),
+    "pc": ("psum", [128, 512], "float32"), "pr": ("psum", [128, 512], "float32"),
+    "pd": ("psum", [128, 512], "float32"), "px": ("psum", [128, 512], "float32"),
+}
+LOADS = ["x", "u", "a", "p", "s", "w", "t", "j"]
+SEMAPHORES = (["qv", "qa", "qt", "qg", "out"] + ["ld" + n for n in LOADS]
+              + [k + str(t) for k in ("xa", "ua", "va", "xl", "ul", "vl") for t in range(STEPS)])
+PSUM = ("pw0", "pw1", "pw2", "ph", "pc", "pr", "pd", "px")
+
+CY, PE, GA, FIX, SYNC = 0.83, 0.42, 1.5, 60.0, 120.0
+LAT_X, LAT_DMA = 8000.0, 2200.0
+PARTS = (("x", "x", 0, V), ("u", "u", 0, V // 2), ("v", "u", V // 2, V // 2))
+TURNS, JITTER, SEED = 20, 0.8, 3
+SCAN = [(1, 2, 3)] * 5
+HALF = 8
+MOVED = [4, 0, 10, 0, 10]
+
+
+def routes(T, topo, core):
+    others = [c for c in T.cores if c != core]
+    near = [c for c in others if topo.may_write(core, c)]
+    far = [c for c in others if c not in near]
+    gates = [c for c in topo.cores_of(core) if c not in T.cores and all(topo.may_write(c, d) for d in far)]
+    same = [c for c in gates if topo.die(c) == topo.die(core)]
+    other = [c for c in gates if c not in same]
+    plan = []
+    for rel in (same[:1] + other[:1], other[:2]):
+        plan.append({r: far[i::len(rel)] for i, r in enumerate(rel)} if far else {})
+    return near, plan
+
+
+def bits(engines):
+    m = 0
+    for e in engines:
+        m |= 1 << e
+    return m
+
+
+def dst(topo, d, src):
+    rid, pid = topo.addr(d, src)
+    return DstId(rid=rid, pnc=pid)
+
+
+def relay_program(g, core, T, topo, owner):
+    q = T.rank_of(owner)
+    near, plan = routes(T, topo, owner)
+    sent = 0
+    for t in range(STEPS):
+        for kind, tab, c0, w in PARTS:
+            rel = plan["xu".index(tab)]
+            if core not in rel:
+                continue
+            far = rel[core]
+            off = topo.engines(core, far[0])
+            n_in = len(own_engines(topo, owner, near, core))
+            sent += len(off)
+            g.wait_ge(T.sem[kind + "a%d" % t], n_in)
+            src = T["t" + tab + "0"][:, t * V + c0:t * V + c0 + w]
+            land = T["t%s%d" % (tab, t % 2)][:, q * V + c0:q * V + c0 + w]
+            g.remote_dma_fused([RemoteDMATransfer(
+                dst_ids=[dst(topo, d, core) for d in far], dma_engine_mask=bits(off),
+                remote_sem=T.sem[kind + "a%d" % t], srcs=[src], dsts=[land for d in far])],
+                local_sem=T.sem.xl0)
+    if sent:
+        g.wait_ge(T.sem.xl0, sent)
+
+
+def own_engines(topo, core, near, relay):
+    off = topo.engines(core, near[0])
+    return [e for e in topo.engines(core, relay) if e not in off]
+
+
+def build(g, core, T, topo):
+    q = T.rank_of(core)
+    near, plan = routes(T, topo, core)
+    ops, tag = [], ["init", -1]
+
+    def op(eng, cost, reads, writes, fn, sem=None, lat=0.0, ext=None):
+        ops.append({"eng": eng, "cost": cost, "r": reads, "w": writes, "fn": fn, "sem": sem, "lat": lat,
+                    "tag": tag[0], "step": tag[1]})
+
+    def R(name, lo=0, n=None):
+        return (name, lo, 1 << 20 if n is None else lo + n)
+
+    def A(reg):
+        name, lo, hi = reg
+        return T[name][:] if hi == 1 << 20 else T[name][:, lo:hi]
+
+    def wid(reg):
+        return reg[2] - reg[1] if reg[2] != 1 << 20 else T[reg[0]].shape[1]
+
+    two = ("sb", "cm", "shm", "trm", "selw", "jd", "tx0", "tx1", "gsel", "i16", "off")
+
+    def sc(x):
+        return A(x) if isinstance(x, tuple) else x
+
+    def ts(out, in0, s1, op0, s2=None, op1=None):
+        fast = out[0] in two and in0[0] in two
+        rd = [in0] + [s for s in (s1, s2) if isinstance(s, tuple)]
+        if op1 is None:
+            fn = lambda: g.vector.tensor_scalar(A(out), A(in0), sc(s1), None, op0)
+        else:
+            fn = lambda: g.vector.tensor_scalar(A(out), A(in0), sc(s1), sc(s2), op0, op1)
+        op("v", FIX + max(64, wid(out) * (0.5 if fast else 1)) * CY, rd, [out], fn)
+
+    def tt(out, in0, in1, alu):
+        k = 1 if in0[0] in PSUM or in1[0] in PSUM else 2
+        op("v", FIX + max(64, wid(out) * k) * CY, [in0, in1], [out],
+           lambda: g.vector.tensor_tensor(A(out), A(in0), A(in1), alu))
+
+    def cp(out, in0):
+        op("v", FIX + max(64, wid(out)) * CY, [in0], [out], lambda: g.vector.tensor_copy(A(out), A(in0)))
+
+    def act(out, in0, func, bias=0.0, scale=1.0):
+        rd = [in0] + [s for s in (bias, scale) if isinstance(s, tuple)]
+        op("a", FIX + max(64, wid(out)) * CY, rd, [out],
+           lambda: g.scalar.activation(A(out), A(in0), func, bias=sc(bias), scale=sc(scale)))
+
+    def mm(items, reads, writes):
+        def fn():
+            last = None
+            for o, l, r, s0, s1, _ in items:
+                last = g.tensor.matmul(o, l, r, s0, s1)
+            return last
+        op("t", 15 + sum(i[5] for i in items) * PE, reads, writes, fn)
+
+    def lin(out, terms, start=True, stop=True):
+        n = len(terms)
+        mm([(A(out), A(m), A(x), start and i == 0, stop and i == n - 1, wid(x)) for i, (m, x) in enumerate(terms)],
+           [m for m, x in terms] + [x for m, x in terms] + ([] if start else [out]), [out])
+
+    def dma(eng, out_ap, in_ap, reads, writes, sem):
+        qq = g.sync if eng == "s" else g.scalar
+        op(eng, 60.0, reads, writes, lambda: qq.dma_start(out_ap, in_ap), sem=sem, lat=LAT_DMA)
+
+    def send(kind, t):
+        kind, tab, c0, w = PARTS["xuv".index(kind)]
+        own = R("t%s%d" % (tab, t % 2), q * V + c0, w)
+        rel = plan["xu".index(tab)]
+        off = topo.engines(core, near[0])
+        on = own_engines(topo, core, near, list(rel)[0])
+        sem = T.sem[kind + "a%d" % t]
+
+        def fn():
+            g.remote_dma_fused([
+                RemoteDMATransfer(dst_ids=[dst(topo, r, core) for r in rel], dma_engine_mask=bits(on), remote_sem=sem,
+                                  srcs=[A(own)], dsts=[T["t" + tab + "0"][:, t * V + c0:t * V + c0 + w] for r in rel]),
+                RemoteDMATransfer(dst_ids=[dst(topo, d, core) for d in near], dma_engine_mask=bits(off), remote_sem=sem,
+                                  srcs=[A(own)], dsts=[A(own) for d in near])],
+                local_sem=T.sem[kind + "l%d" % t])
+            return None
+        op("g", 1000.0, [own], [R("sent" + kind, t, 1), R("turn")], fn, sem=(kind + "l%d" % t, len(on) + len(off)), lat=3000.0)
+        op(None, 0.0, [R("sent" + kind, t, 1)], [R("arr" + kind, t, 1)], None,
+           sem=(kind + "a%d" % t, len(off) * (len(T.cores) - 1)), lat=LAT_X - 4000.0, ext=True)
+
+    SB = lambda i: R("sb", i * V, V)
+    SF = lambda i: R("sf", i * V, V)
+    CM = lambda i: R("cm", i * 128, 128)
+    COL = lambda i: R("col", i, 1)
+    AG, WW, RHO, KEY, FRESH, SS, SW2, XB, WGT, L2 = [SB(i) for i in range(10)]
+    NL, cap, CAP1 = [SB(10), SB(11)], SB(12), SB(13)
+    JJ0, JJC, CPRE, TMP, OX, OC = [SF(i) for i in range(6)]
+    EE, BO, ID, KM, MS, MN, I3, I241, IM15, IM3, IM1, I2 = [CM(i) for i in range(12)]
+    PK, PKH, QF, NB = COL(0), COL(1), COL(2), COL(3)
+    MK, TB = (lambda k: COL(16 + k)), (lambda d: COL(8 + d - 1))
+    DH, DT = R("pd", 0, V), R("pd", V, V)
+    OFF = lambda i: R("off", i * V, V)
+    XO = lambda t: R("tx%d" % (t % 2), q * V, V)
+    UO = lambda t: R("tu%d" % (t % 2), q * V, V)
+    I16TH = R("trm", 7 * 128, 128)
+
+    dma("s", A(XO(0)), T.x0[:], [], [XO(0)], ("ldx", 16))
+    dma("s", A(UO(0)), T.u0[:], [], [UO(0)], ("ldu", 16))
+    dma("a", A(AG), T.ag[:], [], [AG], ("lda", 16))
+    dma("a", T.si[:], T.s0[:], [], [R("si")], ("lds", 16))
+    dma("a", T.cr[:], T.p0[:], [], [R("cr")], ("ldp", 16))
+    dma("a", A(WW), T.w0[:], [], [WW], ("ldw", 16))
+    dma("s", T.jt[:], T.ax[:], [], [R("jt")], ("ldj", 16))
+    dma("s", T.thi[:], T.th[:], [], [R("thi")], ("ldt", 16))
+
+    def iota(name, pattern, base, mult):
+        n = T[name].shape[1]
+        op("g", 130 + 2 * n * CY, [], [R(name)], lambda: g.iota(T[name][:], pattern, base, mult))
+    iota("ia", [[1, 128]], 128, -1)
+    iota("ib", [[16, 8], [0, 16]], 143, -1)
+    iota("ic", [[1, 144]], -15, -1)
+    iota("ip", [[1, 16]], 0, 1)
+    send("x", 0)
+    send("u", 0)
+    send("v", 0)
+    iota("ik", [[0, 8], [1, 16]], 0, 0)
+
+    ts(R("ia"), R("ia"), 15, ALU.bitwise_and)
+    ts(R("ib"), R("ib"), 4, ALU.arith_shift_right)
+    ts(R("ib"), R("ib"), 8.0, ALU.not_equal, 16.0, ALU.mult)
+    tt(EE, R("ia"), R("ib"), ALU.add)
+    ts(BO, EE, 16.0, ALU.is_lt)
+    ts(ID, EE, 0.0, ALU.is_equal)
+    ts(R("col", 16, 16), R("ia", 0, 16), 0.0, ALU.is_equal)
+    for k in range(16):
+        act(R("selw", k * 128, 128), BO, ACT.Copy, scale=MK(k))
+    ts(R("ip"), R("ip"), 15, ALU.bitwise_and)
+    cp(PK, R("ip", 0, 1))
+    ts(PKH, PK, 0.5, ALU.mult)
+    ts(R("col", 8, 8), R("ip", 1, 8), PK, ALU.is_lt, -0.5, ALU.add)
+    ts(R("gsel"), R("ic"), PK, ALU.add, 0.0, ALU.is_equal)
+    ts(R("i16"), ID, 2.0 ** -8, ALU.mult)
+
+    ts(RHO, AG, -1.0, ALU.mult, 4.0, ALU.add)
+    ts(NL[0], AG, 3.0, ALU.is_ge)
+    ts(I3, ID, 3.0, ALU.mult)
+    lin(R("pc", V, V), [(ID, RHO), (I3, NL[0])])
+    tt(WGT, WW, R("pc", V, V), ALU.mult)
+    cp(OFF(2), R("si"))
+    tt(DT, R("si"), R("cr"), ALU.subtract)
+    tt(TMP, DT, NL[0], ALU.mult)
+    ts(DH, DT, 0.5, ALU.mult)
+    tt(R("ci"), TMP, R("cr"), ALU.add)
+    cp(OFF(0), R("ci"))
+
+    for k in range(16):
+        ts(R("jd", k * 128, 128), ID, MK(k), ALU.mult, 8.0, ALU.mult)
+    ts(R("i32", 0, 128), ID, 2.0 ** -11, ALU.mult)
+    ts(R("i32", 128, 128), ID, 0.5, ALU.mult)
+    for m, x in ((I241, 241.0), (IM15, -1.5), (IM3, -3.0), (IM1, -1.0), (I2, 2.0)):
+        act(m, ID, ACT.Copy, scale=x)
+    for name, ds, pb in (("shm", (15, 14, 13, 12), "pw0"), ("shm", (11, 10, 9, 8), "pw1"),
+                         ("trm", (1, 2, 3, 4), "pw2"), ("trm", (5, 6, 7), "px")):
+        c0 = 0 if ds[0] in (15, 1) else 512
+        for i, d in enumerate(ds):
+            m = R(name, c0 + i * 128, 128)
+            ts(m, EE, float(d), ALU.is_equal)
+            lin(R(pb, i * 128, 128), [(ID, m), (IM1, ID)])
+        act(R(name, c0, 128 * len(ds)), R(pb, 0, 128 * len(ds)), ACT.Copy)
+    ts(KM, R("ia"), 0.0, ALU.is_equal)
+    ts(MS, ID, 32.0, ALU.mult)
+    ts(MN, ID, -64.0, ALU.mult)
+    tt(MS, MS, KM, ALU.add)
+    tt(MN, MN, BO, ALU.add)
+    tt(MN, MN, BO, ALU.add)
+    act(I16TH, ID, ACT.Copy, scale=1.0 / 16)
+    act(R("gneg"), R("gsel"), ACT.Copy, scale=-1.0)
+    BOM = {}
+    for m in sorted(set(MOVED) - {0}):
+        BOM[m] = CM(12 + len(BOM))
+        ts(BOM[m], R("ik"), float(16 - m), ALU.is_ge)
+        tt(BOM[m], BOM[m], BO, ALU.mult)
+    op("v", FIX + 512 * CY, [], [R("seg")], lambda: g.vector.memset(T.seg[:], 1.0))
+    op("v", FIX + 64 * CY, [], [R("seg")], lambda: g.vector.memset(T.seg[:, 0:1024:16], 0.0))
+    ts(QF, R("thi", 0, 1), -1.0, ALU.mult, 0.5, ALU.add)
+    ts(NB, R("thi", 1, 1), -1.0, ALU.mult, 0.5, ALU.add)
+
+    def gather_act(out_ap, out_reg, tab, offs, c, extra):
+        o = R("off", offs * V + c * 64, 64)
+        op("a", FIX + 1024 * GA * CY, [R(tab), o] + extra, [out_reg],
+           lambda: g.scalar.activation(out_ap, T[tab][:, 0:WIN].indirect(A(o)), ACT.Copy))
+        ops[-1]["ga"] = 1024
+
+    def jumps(offs, out):
+        for c in range(4):
+            b = (c % 2) * 1024
+            gather_act(T.jg[:, b:b + 1024], R("jg", b, 1024), "jt", offs, c, [])
+            o = R("pr", V + c * 64, 64)
+            mm([(A(o), T.jd[:, k * 128:(k + 1) * 128], T.jg[:, b + k:b + 1024:16], k == 0, k == 15, 64) for k in range(16)],
+               [R("jd"), R("jg", b, 1024)], [o])
+        act(out, R("pr", V, V), ACT.Identity, bias=PKH)
+
+    def select(mask, val):
+        tt(DT, val, DH, ALU.subtract)
+        tt(TMP, DT, mask, ALU.mult)
+        tt(DH, DH, TMP, ALU.add)
+
+    jumps(2, JJ0)
+    select(NL[0], JJ0)
+    rot = [0]
+
+    def bank():
+        rot[0] += 1
+        return ("pw0", "pw1", "pw2", "px")[rot[0] % 4]
+
+    for t in range(STEPS):
+        p, last = t % 2, t == STEPS - 1
+        tx, tu, ws = "tx%d" % p, "tu%d" % p, "ws%d" % p
+        X, U, nl = XO(t), UO(t), NL[p]
+        tag[1], tag[0] = t, "xc"
+        lin(DT, [(ID, X)])
+        for c in range(4):
+            v0 = c * 64
+            tag[0] = "xc"
+            gather_act(T.xc[:, c * 1024:(c + 1) * 1024], R("xc", c * 1024, 1024), tx, p, c, [R("arrx", t, 1)])
+            for h in range(2):
+                b, v1 = bank(), v0 + 32 * h
+                tag[0] = "xw"
+                mm([(T[b][:, k:512:16], T.selw[:, k * 128:(k + 1) * 128], T.sb[:, WGT[1] + v1:WGT[1] + v1 + 32],
+                     True, True, 64) for k in range(16)], [R("selw"), WGT], [R(b)])
+                tt(R("wx", (c % 2) * 1024 + h * 512, 512), R("xc", 16 * v1, 512), R(b), ALU.mult)
+                tag[0] = "ws"
+                act(R(ws, 16 * v1, 512), R(b), ACT.Copy)
+            tag[0] = "xw"
+            o = R("ph", v0, 64)
+            b0 = (c % 2) * 1024
+            mm([(A(o), T.i16[:], T.wx[:, b0 + k:b0 + 1024:16], k == 0, k == 15, 64) for k in range(16)],
+               [R("i16"), R("wx", b0, 1024)], [o])
+        tag[0] = "nx"
+        ts(XB, R("ph", 0, V), 15.0, ALU.min, 128.501953125, ALU.add)
+        XN = XO(t + 1)
+        ts(XN, XB, -129.0, ALU.add)
+        if not last:
+            send("x", t + 1)
+        else:
+            act(OX, XN, ACT.Copy)
+            dma("s", T.yx[:], A(OX), [OX], [], ("out", 16))
+        lin(R("ph", V, V), [(BO, XN)])
+        act(SS, R("ph", V, V), ACT.Sign, bias=NB)
+        C = R("pc", 0, V)
+        tag[0] = "mn"
+        mv = MOVED[t]
+        lin(C, [(I241, nl)] + ([(BOM[mv], X)] if mv else []), stop=False)
+        turn = list(range(16 - mv))
+        for i in range(mv):
+            turn.insert(i * 16 // mv, 16 - mv + i)
+        for i, k in enumerate(turn):
+            o = R("mn", i * V, V)
+            if k < 16 - mv:
+                w = V // 2 if k < HALF else V
+                for v0 in range(0, V, w):
+                    o2, x2 = R("mn", i * V + v0, w), R("pd", V + v0, w)
+                    op("v", FIX + w * CY, [R("xc", 16 * v0, 16 * w), x2], [o2],
+                       lambda o2=o2, x2=x2, k=k, v0=v0, w=w: g.vector.tensor_tensor(
+                           A(o2), T.xc[:, 16 * v0 + k:16 * (v0 + w):16], A(x2), ALU.min))
+                lin(C, [(R("gsel", 15 - k, 128), o)], start=False, stop=i == 15)
+            else:
+                d = R(bank(), 0, V)
+                mm([(A(d), A(ID), A(X), True, False, V), (A(d), A(IM1), T.xc[:, k:16 * V:16], False, True, V)],
+                   [ID, IM1, X, R("xc")], [d])
+                act(o, d, ACT.Relu)
+                lin(C, [(R("gneg", 15 - k, 128), o)], start=False, stop=i == 15)
+        tag[0] = "tail"
+        act(KEY, C, ACT.Identity, bias=R("col", 4, 1))
+        act(FRESH, KEY, ACT.Sign, bias=QF)
+        Z = R("pc", V, V)
+        first = True
+        for d2 in range(4):
+            b = bank()
+            for i in range(2):
+                d = 2 * d2 + i + 1
+                lin(R(b, i * V, V), [(R("shm", (d - 1) * 128, 128), KEY)])
+            for i in range(2):
+                d = 2 * d2 + i + 1
+                act(R("sg", (d - 1) * V, V), R(b, i * V, V), ACT.Sign, bias=TB(d))
+            terms = [(R("trm", (d - 1) * 128, 128) if d < 8 else IM1, R("sg", (d - 1) * V, V)) for d in (2 * d2 + 1, 2 * d2 + 2)]
+            if first:
+                terms = [(MN, nl), (MS, SS)] + terms
+            lin(Z, terms, start=first, stop=d2 == 3)
+            first = False
+        act(cap, Z, ACT.Sign, bias=R("col", 7, 1))
+        if t in (1, 3):
+            tag[0] = "j"
+            ts(CAP1, cap, 0.0, ALU.is_gt)
+            jumps(p, JJC)
+            select(nl, JJC)
+        tag[0] = "l"
+        if t == 1:
+            ts(L2, RHO, 2.0, ALU.is_equal)
+        tag[0] = "m"
+        if t == 2:
+            select(L2, JJ0)
+        tag[0] = "s"
+        if t in (2, 4):
+            select(CAP1, JJC)
+        tag[0] = "end"
+        tt(CPRE, R("ci"), DH, ALU.add)
+        lin(R("ph", 0, V), [(IM1, RHO), (IM3, nl), (ID, FRESH)], stop=False)
+        lin(R("ph", 0, V), [(IM1, cap)], start=False)
+        act(SW2, R("ph", 0, V), ACT.Sign, bias=R("col", 5, 1), scale=-1.0)
+        tt(DH, DH, SW2, ALU.mult)
+        tt(R("cr"), CPRE, DH, ALU.subtract)
+        ts(R("ci"), R("cr"), WIN - 1, ALU.bitwise_and)
+        if not last:
+            cp(OFF(1 - p), R("ci"))
+        else:
+            cp(OC, R("ci"))
+            dma("s", T.yc[:], A(OC), [OC], [], ("out", 16))
+        lin(R("ph", V, V), [(ID, RHO), (I2, FRESH), (IM15, cap)])
+        ts(RHO, R("ph", V, V), -0.5, ALU.add, 1.0, ALU.max)
+        lin(R("pc", 0, V), [(ID, WW), (I2, cap)])
+        ts(WW, R("pc", 0, V), 2.0, ALU.add, 15.0, ALU.min)
+        if not last:
+            ts(NL[1 - p], RHO, 2.0, ALU.is_lt)
+            lin(R("pc", V, V), [(ID, RHO), (I3, NL[1 - p])])
+            tt(WGT, WW, R("pc", V, V), ALU.mult)
+        else:
+            ts(DT, RHO, -16.0, ALU.mult, 64.0, ALU.add)
+            tt(JJ0, DT, WW, ALU.add)
+            dma("s", T.yw[:], A(JJ0), [JJ0], [], ("out", 16))
+        tag[0] = "u"
+        for c in range(4):
+            v0, b0 = c * 64, (c % 2) * 1024
+            for h in range(2):
+                v1, b1 = v0 + 32 * h, b0 + 512 * h
+                o = R("off", p * V + v1, 32)
+                op("v", FIX + 512 * GA * CY, [R(tu), o, R(ws, 16 * v1, 512), R("arru", t, 1), R("arrv", t, 1)], [R("wu", b1, 512)],
+                   lambda o=o, b1=b1, v1=v1, tu=tu, ws=ws: g.vector.tensor_tensor(
+                       T.wu[:, b1:b1 + 512], T[tu][:, 0:WIN].indirect(A(o)), T[ws][:, 16 * v1:16 * v1 + 512], ALU.mult))
+                ops[-1]["ga"] = 512
+            r = R("pr", v0, 64)
+            items = ([(A(r), A(I16TH), T[tx][:, q * V + v0:q * V + v0 + 64], True, False, 64),
+                      (A(r), T.i32[:, 128:256], T[tu][:, q * V + v0:q * V + v0 + 64], False, False, 256)]
+                     + [(A(r), T.i32[:, 0:128], T.wu[:, b0 + k:b0 + 1024:16], False, k == 15, 256) for k in range(16)])
+            if c in SCAN[t]:
+                op("v", FIX + 1024 * CY, [R("seg"), R("wu", b0, 1024)], [R("su")],
+                   lambda b0=b0: g.vector.tensor_tensor_scan(T.su[:], T.seg[:], T.wu[:, b0:b0 + 1024], 0.0, ALU.mult, ALU.add))
+                mm(items[:2] + [(A(r), T.i32[:, 0:128], T.su[:, 15:1024:16], False, True, 256)],
+                   [I16TH, R("i32"), X, U, R("su")], [r])
+            for i in range(0, 0 if c in SCAN[t] else 18, 3):
+                mm(items[i:i + 3], [I16TH, R("i32"), X, U, R("wu", b0, 1024)], [r])
+            if c % 2:
+                c0 = v0 - 64
+                un = R(UO(t + 1)[0], q * V + c0, 128)
+                act(un, R("pr", c0, 128), ACT.Tanh, bias=R("col", 6, 1))
+                if not last:
+                    send("uv"[c // 2], t + 1)
+                else:
+                    dma("s", T.yu[:, c0:c0 + 128], A(un), [un], [], ("out", 16))
+
+    head = []
+    for i, x in ((4, -241.0), (5, -2.5), (6, -0.5), (7, -39.5)):
+        head.append({"eng": "v", "cost": 110.0, "r": [], "w": [COL(i)], "sem": None, "lat": 0.0, "tag": "init", "step": -1,
+                     "fn": lambda i=i, x=x: g.vector.memset(A(COL(i)), x)})
+    return head + ops
+
+
+def meet(a, b):
+    return a[0] == b[0] and a[1] < b[2] and b[1] < a[2]
+
+
+def depend(ops):
+    n = len(ops)
+    deps = [set() for _ in range(n)]
+    seen = {}
+    for i, o in enumerate(ops):
+        for reg, wr in [(x, False) for x in o["r"]] + [(x, True) for x in o["w"]]:
+            for j, reg2, wr2 in seen.get(reg[0], []):
+                if j != i and (wr or wr2) and meet(reg, reg2):
+                    deps[i].add(j)
+            if wr and o["eng"] == "t" and reg[0] in ("pc", "ph", "pr"):
+                deps[i].update(j for j, reg2, wr2 in seen.get(reg[0], []) if j != i and wr2)
+        for reg, wr in [(x, False) for x in o["r"]] + [(x, True) for x in o["w"]]:
+            seen.setdefault(reg[0], []).append((i, reg, wr))
+    return deps
+
+
+def place(ops, pred, rank, back):
+    start, busy = {}, {}
+    for i in sorted(range(len(ops)), key=lambda i: rank[i]):
+        o, s = ops[i], 0.0
+        e, c = o["eng"], o["cost"]
+        for j in pred[i]:
+            f = ops[j]["eng"]
+            gap = SYNC if f != e else 0.0 if e == "t" else 60.0
+            lat = 0.0 if e == f == "g" else o["lat"] if back else ops[j]["lat"]
+            s = max(s, start[j] + ops[j]["cost"] + lat + gap)
+        if back and not pred[i]:
+            s = o["lat"]
+        res = ([e] if e else []) + o["banks"]
+        again = True
+        while again:
+            again = False
+            for r in res:
+                lst = busy.setdefault(r, [])
+                lo, hi = 0, len(lst)
+                while lo < hi:
+                    mid = (lo + hi) // 2
+                    if lst[mid][1] + SYNC <= s:
+                        lo = mid + 1
+                    else:
+                        hi = mid
+                for a, b, f in lst[lo:]:
+                    m = 0.0 if f == e else SYNC
+                    if a - m >= s + c:
+                        break
+                    if b + m > s:
+                        s, again = b + m, True
+        start[i] = s
+        for r in res:
+            busy[r].append((s, s + c, e))
+            busy[r].sort()
+    return [start[i] for i in range(len(ops))]
+
+
+def times(ops, deps, succ, seed):
+    n = len(ops)
+    level = [0.0] * n
+    for i in range(n - 1, -1, -1):
+        level[i] = ops[i]["cost"] + ops[i]["lat"] + 1.0 + max([level[j] for j in succ[i]] + [0.0])
+    rank, best = [-x for x in level], None
+    for turn in range(TURNS):
+        at = place(ops, deps, rank, False)
+        end = max(at[i] + ops[i]["cost"] + ops[i]["lat"] for i in range(n))
+        if best is None or end < best[0]:
+            best = (end, at)
+        rank = [0.0] * n
+        for i in range(n - 1, -1, -1):
+            seed = (seed * 1103515245 + 12345) % 2147483648
+            rank[i] = max([-at[i] - ops[i]["cost"] + (seed % 1000) * JITTER] + [rank[j] + 0.001 for j in succ[i]])
+        bt = place(ops, succ, rank, True)
+        rank = [0.0] * n
+        for i in range(n):
+            rank[i] = max([-bt[i] - ops[i]["cost"]] + [rank[j] + 0.001 for j in deps[i]])
+    return best[1]
+
+
+def schedule(ops, seed):
+    n = len(ops)
+    deps = depend(ops)
+    succ = [[] for _ in range(n)]
+    for i in range(n):
+        ops[i]["banks"] = sorted(set(x[0] for x in ops[i]["r"] + ops[i]["w"] if x[0] in PSUM))
+        for j in deps[i]:
+            succ[j].append(i)
+    key = times(ops, deps, succ, seed)
+    for i in range(n):
+        ops[i]["at"] = key[i]
+    left = [len(d) for d in deps]
+    ready = [i for i in range(n) if left[i] == 0]
+    used, order = {}, []
+    while ready:
+        i = min(ready, key=lambda i: (key[i], i))
+        e = ops[i]["eng"]
+        for b in set(x[0] for x in ops[i]["r"] + ops[i]["w"] if x[0] in PSUM):
+            deps[i].update(j for e2, j in used.get(b, {}).items() if e2 != e)
+            used.setdefault(b, {})[e] = i
+        order.append(i)
+        ready.remove(i)
+        for j in succ[i]:
+            left[j] -= 1
+            if left[j] == 0:
+                ready.append(j)
+    return order, deps
+
+
+PLAN = {}
+
+
+def rank_program(g, core, T, topo):
+    if T.rank_of(core) is None:
+        for owner in topo.cores_of(core):
+            if T.rank_of(owner) is not None:
+                relay_program(g, core, T, topo, owner)
+        return
+    ops = build(g, core, T, topo)
+    if "order" not in PLAN:
+        PLAN["order"], PLAN["deps"] = schedule(ops, SEED)
+    order, deps = PLAN["order"], PLAN["deps"]
+    queue = {"v": g.vector, "a": g.scalar, "t": g.tensor, "g": g, "s": g.sync}
+    needed = set(j for i in order for j in deps[i] if ops[i]["eng"] is not None
+                 and not (ops[i]["eng"] == "t" and ops[j]["eng"] == "t"))
+    count, token, waited, total = {}, {}, {}, {}
+    for i in order:
+        o = ops[i]
+        e = o["eng"]
+        if e is not None:
+            want = {}
+            for j in deps[i]:
+                if j in token and not (e == "t" and ops[j]["eng"] == "t"):
+                    s, x = token[j]
+                    want[s] = max(want.get(s, 0), x)
+            for s in sorted(want):
+                if waited.get((e, s), 0) < want[s]:
+                    queue[e].wait_ge(T.sem[s], want[s])
+                    waited[(e, s)] = want[s]
+        ins = o["fn"]() if o["fn"] else None
+        if o["sem"]:
+            s, x = o["sem"]
+            if ins is not None:
+                ins.then_inc(T.sem[s], x)
+            total[s] = total.get(s, 0) + x
+            token[i] = (s, total[s])
+        elif i in needed:
+            s = "q" + e
+            ins.then_inc(T.sem[s], 1)
+            total[s] = total.get(s, 0) + 1
+            token[i] = (s, total[s])
+    for s in sorted(total):
+        if not any(waited.get((e, s), 0) >= total[s] for e in queue):
+            g.wait_ge(T.sem[s], total[s])

@@ -4,33 +4,37 @@ from concourse.mybir import AluOpType, ActivationFunctionType
 ALU = AluOpType
 ACT = ActivationFunctionType
 STEPS, V, WIN = 5, 256, 2048
+H = V // 2
 
 SCRATCH = {
     "tx0": ("sbuf", [128, WIN], "bfloat16"), "tx1": ("sbuf", [128, WIN], "bfloat16"),
+    "tx2": ("sbuf", [128, WIN], "bfloat16"),
     "tu0": ("sbuf", [128, WIN], "float32"), "tu1": ("sbuf", [128, WIN], "float32"),
+    "wd00": ("dram", [8, 2, 16 * H], "bfloat16"), "wd01": ("dram", [8, 2, 16 * H], "bfloat16"),
+    "wd10": ("dram", [8, 2, 16 * H], "bfloat16"), "wd11": ("dram", [8, 2, 16 * H], "bfloat16"),
     "jt": ("sbuf", [128, WIN], "bfloat16"),
     "xc": ("sbuf", [128, 16 * V], "bfloat16"),
     "ws0": ("sbuf", [128, 16 * V], "bfloat16"), "ws1": ("sbuf", [128, 16 * V], "bfloat16"),
-    "wx": ("sbuf", [128, 2048], "float16"),
+    "wx": ("sbuf", [128, 4096], "float16"),
     "mn": ("sbuf", [128, 4096], "bfloat16"),
-    "wu": ("sbuf", [128, 2048], "float32"),
-    "jg": ("sbuf", [128, 2048], "bfloat16"),
+    "wu": ("sbuf", [128, 4096], "float32"),
+    "jg": ("sbuf", [128, 4096], "bfloat16"),
     "sg": ("sbuf", [128, 2048], "bfloat16"),
+    "zr": ("sbuf", [128, 1024], "bfloat16"),
     "selw": ("sbuf", [128, 2048], "bfloat16"), "jd": ("sbuf", [128, 2048], "bfloat16"),
     "shm": ("sbuf", [128, 1024], "bfloat16"), "trm": ("sbuf", [128, 1024], "bfloat16"),
-    "cm": ("sbuf", [128, 128 * 15], "bfloat16"),
+    "cm": ("sbuf", [128, 128 * 18], "bfloat16"), "bw": ("sbuf", [128, 512], "bfloat16"),
     "gsel": ("sbuf", [128, 144], "bfloat16"), "gneg": ("sbuf", [128, 144], "bfloat16"),
-    "seg": ("sbuf", [128, 1024], "bfloat16"), "su": ("sbuf", [128, 1024], "float32"),
-    "ik": ("sbuf", [128, 128], "int32"),
+    "seg": ("sbuf", [128, 1024], "bfloat16"), "su": ("sbuf", [128, 2048], "float32"),
     "i16": ("sbuf", [128, 128], "float16"),
     "i32": ("sbuf", [128, 256], "float32"),
     "ia": ("sbuf", [128, 128], "int32"), "ib": ("sbuf", [128, 128], "int32"), "ic": ("sbuf", [128, 144], "int32"),
     "ip": ("sbuf", [128, 16], "int32"),
-    "col": ("sbuf", [128, 48], "float32"),
+    "col": ("sbuf", [128, 40], "float32"),
     "thi": ("sbuf", [128, 2], "int32"),
     "si": ("sbuf", [128, V], "int32"), "ci": ("sbuf", [128, V], "int32"), "cr": ("sbuf", [128, V], "int32"),
-    "off": ("sbuf", [128, 3 * V], "uint16"),
-    "sb": ("sbuf", [128, 16 * V], "bfloat16"),
+    "off": ("sbuf", [128, 6 * V], "uint16"),
+    "sb": ("sbuf", [128, 17 * V], "bfloat16"),
     "sf": ("sbuf", [128, 6 * V], "float32"),
     "pw0": ("psum", [128, 512], "float32"), "pw1": ("psum", [128, 512], "float32"),
     "pw2": ("psum", [128, 512], "float32"), "ph": ("psum", [128, 512], "float32"),
@@ -39,16 +43,29 @@ SCRATCH = {
 }
 LOADS = ["x", "u", "a", "p", "s", "w", "t", "j"]
 SEMAPHORES = (["qv", "qa", "qt", "qg", "out"] + ["ld" + n for n in LOADS]
-              + [k + str(t) for k in ("xa", "ua", "va", "xl", "ul", "vl") for t in range(STEPS)])
-PSUM = ("pw0", "pw1", "pw2", "ph", "pc", "pr", "pd", "px")
+              + [k + str(t) for k in ("xa", "ya", "ua", "va", "xl", "yl", "ul", "vl") for t in range(STEPS)]
+              + ["%s%d%d" % (k, t, h) for k in ("wd", "wi") for t in range(STEPS) for h in range(2)])
+PSUM = ("ph", "pc", "pr", "pd")
+LENT = ("pw0", "pw1", "pw2", "px")
 
 CY, PE, GA, FIX, SYNC = 0.83, 0.42, 1.5, 60.0, 120.0
-LAT_X, LAT_DMA = 8000.0, 2200.0
-PARTS = (("x", "x", 0, V), ("u", "u", 0, V // 2), ("v", "u", V // 2, V // 2))
-TURNS, JITTER, SEED = 20, 0.8, 3
+LAT_X, LAT_U, LAT_DMA, LAT_T, LAT_W = 8000.0, 8500.0, 2200.0, 3000.0, 5000.0
+TURNS, JITTER, SEED, HASTE, EARLY, DRIFT = 300, 1500.0, 3, 8.0, 200.0, 1000.0
+RUSH = {}
+FENCES = []
+PERIOD, URGE, LATE, SLOW, CARE = 17.3, 10.0, 3000.0, 1.6, 0.3
+PHASES = {"wd": (-5, -4), "xc": (0, 1), "xw": (0.5, 1.5), "nx": (2, 2.5), "ws": (3, 4), "mn": (5, 8), "tail": (6, 9),
+          "j": (6.5, 9.5), "end": (7, 10), "u": (11, 12)}
 SCAN = [(1, 2, 3)] * 5
-HALF = 8
-MOVED = [4, 0, 10, 0, 10]
+MOVED = [8, 4, 8, 4, 8]
+XV = [()] * 5
+JV = [(), (), ()]
+BYDMA = [(0, 1)] * 5
+WIDE = ()
+XH, XNA = False, True
+NLA = True
+UW = 1024
+SELG = ()
 
 
 def routes(T, topo, core):
@@ -58,10 +75,19 @@ def routes(T, topo, core):
     gates = [c for c in topo.cores_of(core) if c not in T.cores and all(topo.may_write(c, d) for d in far)]
     same = [c for c in gates if topo.die(c) == topo.die(core)]
     other = [c for c in gates if c not in same]
-    plan = []
-    for rel in (same[:1] + other[:1], other[:2]):
-        plan.append({r: far[i::len(rel)] for i, r in enumerate(rel)} if far else {})
+    plan = [{r: far[i::len(rel)] for i, r in enumerate(rel)} for rel in (other[:2], same[:2])]
+    spare = [c for c in topo.cores_of(core) if c not in gates and topo.die(c) != topo.die(core)]
+    plan[1][spare[0]] = near
     return near, plan
+
+
+def parts(t):
+    x = {"x": ("x", 0, H), "y": ("x", H, H)} if t and XH else {"x": ("x", 0, V)}
+    return {**x, "u": ("u", 0, H), "v": ("u", H, H)}
+
+
+def table(tab, t):
+    return "t%s%d" % (tab, t % (3 if tab == "x" else 2))
 
 
 def bits(engines):
@@ -81,17 +107,16 @@ def relay_program(g, core, T, topo, owner):
     near, plan = routes(T, topo, owner)
     sent = 0
     for t in range(STEPS):
-        for kind, tab, c0, w in PARTS:
+        for kind, (tab, c0, w) in parts(t).items():
             rel = plan["xu".index(tab)]
             if core not in rel:
                 continue
             far = rel[core]
             off = topo.engines(core, far[0])
-            n_in = len(own_engines(topo, owner, near, core))
             sent += len(off)
-            g.wait_ge(T.sem[kind + "a%d" % t], n_in)
+            g.wait_ge(T.sem[kind + "a%d" % t], len(own_engines(topo, owner, near, core, tab)))
             src = T["t" + tab + "0"][:, t * V + c0:t * V + c0 + w]
-            land = T["t%s%d" % (tab, t % 2)][:, q * V + c0:q * V + c0 + w]
+            land = T[table(tab, t)][:, q * V + c0:q * V + c0 + w]
             g.remote_dma_fused([RemoteDMATransfer(
                 dst_ids=[dst(topo, d, core) for d in far], dma_engine_mask=bits(off),
                 remote_sem=T.sem[kind + "a%d" % t], srcs=[src], dsts=[land for d in far])],
@@ -100,31 +125,36 @@ def relay_program(g, core, T, topo, owner):
         g.wait_ge(T.sem.xl0, sent)
 
 
-def own_engines(topo, core, near, relay):
-    off = topo.engines(core, near[0])
+def own_engines(topo, core, near, relay, tab):
+    off = topo.engines(core, near[0]) if tab == "x" else []
     return [e for e in topo.engines(core, relay) if e not in off]
 
 
-def build(g, core, T, topo):
+def build(g, core, T, topo, banks):
     q = T.rank_of(core)
     near, plan = routes(T, topo, core)
-    ops, tag = [], ["init", -1]
+    ops, tag = [], ["init", -1, 0]
 
-    def op(eng, cost, reads, writes, fn, sem=None, lat=0.0, ext=None):
+    def op(eng, cost, reads, writes, fn, sem=None, lat=0.0, remote=False, adds=None):
         ops.append({"eng": eng, "cost": cost, "r": reads, "w": writes, "fn": fn, "sem": sem, "lat": lat,
-                    "tag": tag[0], "step": tag[1]})
+                    "tag": tag[0], "step": tag[1], "half": tag[2], "remote": remote, "adds": adds})
 
     def R(name, lo=0, n=None):
-        return (name, lo, 1 << 20 if n is None else lo + n)
+        return (name, lo, lo + (T[name].shape[1] if n is None else n))
+
+    def B(name):
+        return T[banks.get(name, LENT[0]) if name[0] == "~" else name]
 
     def A(reg):
-        name, lo, hi = reg
-        return T[name][:] if hi == 1 << 20 else T[name][:, lo:hi]
+        return B(reg[0])[:, reg[1]:reg[2]]
 
     def wid(reg):
-        return reg[2] - reg[1] if reg[2] != 1 << 20 else T[reg[0]].shape[1]
+        return reg[2] - reg[1]
 
-    two = ("sb", "cm", "shm", "trm", "selw", "jd", "tx0", "tx1", "gsel", "i16", "off")
+    def half(reg, h):
+        return (reg[0], reg[1] + h * H, reg[1] + h * H + H)
+
+    two = ("sb", "cm", "shm", "trm", "selw", "jd", "tx0", "tx1", "tx2", "zr", "gsel", "gneg", "i16", "off")
 
     def sc(x):
         return A(x) if isinstance(x, tuple) else x
@@ -139,91 +169,106 @@ def build(g, core, T, topo):
         op("v", FIX + max(64, wid(out) * (0.5 if fast else 1)) * CY, rd, [out], fn)
 
     def tt(out, in0, in1, alu):
-        k = 1 if in0[0] in PSUM or in1[0] in PSUM else 2
+        k = 1 if any(x[0] in PSUM or x[0][0] == "~" for x in (in0, in1)) else 2
         op("v", FIX + max(64, wid(out) * k) * CY, [in0, in1], [out],
            lambda: g.vector.tensor_tensor(A(out), A(in0), A(in1), alu))
 
     def cp(out, in0):
         op("v", FIX + max(64, wid(out)) * CY, [in0], [out], lambda: g.vector.tensor_copy(A(out), A(in0)))
 
+    def fill(out, x):
+        op("v", FIX + max(64, wid(out) * 0.5) * CY, [], [out], lambda: g.vector.memset(A(out), x))
+
     def act(out, in0, func, bias=0.0, scale=1.0):
         rd = [in0] + [s for s in (bias, scale) if isinstance(s, tuple)]
         op("a", FIX + max(64, wid(out)) * CY, rd, [out],
            lambda: g.scalar.activation(A(out), A(in0), func, bias=sc(bias), scale=sc(scale)))
 
-    def mm(items, reads, writes):
+    def mm(items, reads, writes, adds=None):
         def fn():
             last = None
             for o, l, r, s0, s1, _ in items:
                 last = g.tensor.matmul(o, l, r, s0, s1)
             return last
-        op("t", 15 + sum(i[5] for i in items) * PE, reads, writes, fn)
+        op("t", 15 + sum(i[5] for i in items) * PE, reads, writes, fn, adds=adds)
+        ops[-1]["calls"] = len(items)
 
     def lin(out, terms, start=True, stop=True):
         n = len(terms)
         mm([(A(out), A(m), A(x), start and i == 0, stop and i == n - 1, wid(x)) for i, (m, x) in enumerate(terms)],
-           [m for m, x in terms] + [x for m, x in terms] + ([] if start else [out]), [out])
+           [m for m, x in terms] + [x for m, x in terms], [out], adds=None if start or stop else (out, tag[1]))
 
-    def dma(eng, out_ap, in_ap, reads, writes, sem):
+    def dma(eng, out_ap, in_ap, reads, writes, sem, lat=LAT_DMA):
         qq = g.sync if eng == "s" else g.scalar
-        op(eng, 60.0, reads, writes, lambda: qq.dma_start(out_ap, in_ap), sem=sem, lat=LAT_DMA)
+        op(eng, 60.0, reads, writes, lambda: qq.dma_start(out_ap, in_ap), sem=sem, lat=lat)
+
+    def iota(name, pattern, base, mult):
+        n = T[name].shape[1]
+        op("g", 130 + 2 * n * CY, [], [R(name)], lambda: g.iota(T[name][:], pattern, base, mult))
+
+    def pick(out, in0, pattern, base, x, mult=1, keep=ALU.not_equal):
+        op("g", 170 + 2 * wid(out) * CY, [in0], [out],
+           lambda: g.affine_select(A(out), A(in0), pattern, keep, x, base, mult))
 
     def send(kind, t):
-        kind, tab, c0, w = PARTS["xuv".index(kind)]
-        own = R("t%s%d" % (tab, t % 2), q * V + c0, w)
+        tab, c0, w = parts(t)[kind]
+        own = R(table(tab, t), q * V + c0, w)
         rel = plan["xu".index(tab)]
         off = topo.engines(core, near[0])
-        on = own_engines(topo, core, near, list(rel)[0])
+        on = own_engines(topo, core, near, list(rel)[0], tab)
         sem = T.sem[kind + "a%d" % t]
 
         def fn():
-            g.remote_dma_fused([
-                RemoteDMATransfer(dst_ids=[dst(topo, r, core) for r in rel], dma_engine_mask=bits(on), remote_sem=sem,
-                                  srcs=[A(own)], dsts=[T["t" + tab + "0"][:, t * V + c0:t * V + c0 + w] for r in rel]),
-                RemoteDMATransfer(dst_ids=[dst(topo, d, core) for d in near], dma_engine_mask=bits(off), remote_sem=sem,
-                                  srcs=[A(own)], dsts=[A(own) for d in near])],
-                local_sem=T.sem[kind + "l%d" % t])
+            hops = [RemoteDMATransfer(dst_ids=[dst(topo, r, core) for r in rel], dma_engine_mask=bits(on), remote_sem=sem,
+                                      srcs=[A(own)], dsts=[T["t" + tab + "0"][:, t * V + c0:t * V + c0 + w] for r in rel])]
+            if tab == "x":
+                hops.append(RemoteDMATransfer(dst_ids=[dst(topo, d, core) for d in near], dma_engine_mask=bits(off),
+                                              remote_sem=sem, srcs=[A(own)], dsts=[A(own) for d in near]))
+            g.remote_dma_fused(hops, local_sem=T.sem[kind + "l%d" % t])
             return None
-        op("g", 1000.0, [own], [R("sent" + kind, t, 1), R("turn")], fn, sem=(kind + "l%d" % t, len(on) + len(off)), lat=3000.0)
+        hold = [R("sentx", 0, 1)] if (kind, t) == ("u", 0) else []
+        op("g", 1000.0, [own] + hold, [R("sent" + kind, t, 1), R("turn" + tab, 0, 1)], fn,
+           sem=(kind + "l%d" % t, len(on) + (len(off) if tab == "x" else 0)), lat=3000.0, remote=tab)
         op(None, 0.0, [R("sent" + kind, t, 1)], [R("arr" + kind, t, 1)], None,
-           sem=(kind + "a%d" % t, len(off) * (len(T.cores) - 1)), lat=LAT_X - 4000.0, ext=True)
+           sem=(kind + "a%d" % t, len(off) * (len(T.cores) - 1)), lat=(LAT_X if tab == "x" else LAT_U) - 4000.0)
 
     SB = lambda i: R("sb", i * V, V)
     SF = lambda i: R("sf", i * V, V)
     CM = lambda i: R("cm", i * 128, 128)
     COL = lambda i: R("col", i, 1)
-    AG, WW, RHO, KEY, FRESH, SS, SW2, XB, WGT, L2 = [SB(i) for i in range(10)]
-    NL, cap, CAP1 = [SB(10), SB(11)], SB(12), SB(13)
+    AG, WW, R1, KEY, FRESH, SS, SW2, XB, WGT, L2 = [SB(i) for i in range(10)]
+    NL, CAP, CAP1, ONES, WT = [SB(10), SB(11)], SB(12), SB(13), SB(14), [SB(15), SB(16)]
     JJ0, JJC, CPRE, TMP, OX, OC = [SF(i) for i in range(6)]
-    EE, BO, ID, KM, MS, MN, I3, I241, IM15, IM3, IM1, I2 = [CM(i) for i in range(12)]
+    EE, BO, ID, KM, MS, MN, I3, I241, IM15, IM3, IM1, I2, I16TH = [CM(i) for i in range(13)]
     PK, PKH, QF, NB = COL(0), COL(1), COL(2), COL(3)
-    MK, TB = (lambda k: COL(16 + k)), (lambda d: COL(8 + d - 1))
+    TB = lambda d: COL(8 + d - 1)
     DH, DT = R("pd", 0, V), R("pd", V, V)
     OFF = lambda i: R("off", i * V, V)
-    XO = lambda t: R("tx%d" % (t % 2), q * V, V)
-    UO = lambda t: R("tu%d" % (t % 2), q * V, V)
-    I16TH = R("trm", 7 * 128, 128)
+    XO = lambda t: R(table("x", t), q * V, V)
+    UO = lambda t: R(table("u", t), q * V, V)
+    ZR = lambda n: R("zr", 0, n)
+    HB = lambda h, i: R(("pc", "ph")[h], i * H, H)
+    DIAG = [[-1, 128]]
+
+    for i, x in ((4, -241.0), (5, -1.5), (6, -0.5), (7, -39.5), (32, -129.0)):
+        fill(COL(i), x)
+    fill(R("zr"), 0.0)
+    fill(ONES, 1.0)
 
     dma("s", A(XO(0)), T.x0[:], [], [XO(0)], ("ldx", 16))
-    dma("s", A(UO(0)), T.u0[:], [], [UO(0)], ("ldu", 16))
     dma("a", A(AG), T.ag[:], [], [AG], ("lda", 16))
+    dma("a", A(WW), T.w0[:], [], [WW], ("ldw", 16))
     dma("a", T.si[:], T.s0[:], [], [R("si")], ("lds", 16))
     dma("a", T.cr[:], T.p0[:], [], [R("cr")], ("ldp", 16))
-    dma("a", A(WW), T.w0[:], [], [WW], ("ldw", 16))
-    dma("s", T.jt[:], T.ax[:], [], [R("jt")], ("ldj", 16))
-    dma("s", T.thi[:], T.th[:], [], [R("thi")], ("ldt", 16))
-
-    def iota(name, pattern, base, mult):
-        n = T[name].shape[1]
-        op("g", 130 + 2 * n * CY, [], [R(name)], lambda: g.iota(T[name][:], pattern, base, mult))
+    dma("s", T.jt[:], T.ax[:], [], [R("jt")], ("ldj", 16), lat=LAT_DMA + 1000.0)
+    dma("s", A(UO(0)), T.u0[:], [], [UO(0)], ("ldu", 16), lat=LAT_DMA + 1000.0)
+    dma("s", T.thi[:], T.th[:], [], [R("thi")], ("ldt", 16), lat=LAT_DMA + 1000.0)
     iota("ia", [[1, 128]], 128, -1)
     iota("ib", [[16, 8], [0, 16]], 143, -1)
     iota("ic", [[1, 144]], -15, -1)
     iota("ip", [[1, 16]], 0, 1)
-    send("x", 0)
-    send("u", 0)
-    send("v", 0)
-    iota("ik", [[0, 8], [1, 16]], 0, 0)
+    for kind in parts(0):
+        send(kind, 0)
 
     ts(R("ia"), R("ia"), 15, ALU.bitwise_and)
     ts(R("ib"), R("ib"), 4, ALU.arith_shift_right)
@@ -231,238 +276,279 @@ def build(g, core, T, topo):
     tt(EE, R("ia"), R("ib"), ALU.add)
     ts(BO, EE, 16.0, ALU.is_lt)
     ts(ID, EE, 0.0, ALU.is_equal)
+    for m, x in ((I3, 3.0), (I241, 241.0), (IM15, -1.5), (IM3, -3.0), (IM1, -1.0), (I2, 2.0), (I16TH, 1.0 / 16)):
+        ts(m, ID, x, ALU.mult)
+    for c in range(2 if any(BYDMA) else 0):
+        for y in range(2):
+            pick(R("bw", (2 * c + y) * 128, 128), ZR(128), [[-32, 4], [256, 2], [-1, 16]], -16 * c - 256 * y, 1.0)
     ts(R("col", 16, 16), R("ia", 0, 16), 0.0, ALU.is_equal)
-    for k in range(16):
-        act(R("selw", k * 128, 128), BO, ACT.Copy, scale=MK(k))
+    for h in range(2):
+        if h in SELG:
+            pick(R("selw", h * 1024, 1024), ZR(1024), [[-2, 8], [-16, 8], [0, 16]], -h, 1.0)
+        else:
+            for i in range(8):
+                act(R("selw", h * 1024 + i * 128, 128), BO, ACT.Copy, scale=COL(16 + 2 * i + h))
+        pick(R("jd", h * 1024, 1024), ZR(1024), [[-256, 8], [-16, 8], [255, 16]], -2048 * h, 8.0)
+    pick(R("seg"), ZR(1024), [[0, 64], [1, 16]], 0, 1.0, mult=0, keep=ALU.is_equal)
     ts(R("ip"), R("ip"), 15, ALU.bitwise_and)
     cp(PK, R("ip", 0, 1))
     ts(PKH, PK, 0.5, ALU.mult)
     ts(R("col", 8, 8), R("ip", 1, 8), PK, ALU.is_lt, -0.5, ALU.add)
     ts(R("gsel"), R("ic"), PK, ALU.add, 0.0, ALU.is_equal)
+    ts(R("gneg"), R("gsel"), -1.0, ALU.mult)
     ts(R("i16"), ID, 2.0 ** -8, ALU.mult)
+    ts(R("i32", 0, 128), ID, 2.0 ** -11, ALU.mult)
+    ts(R("i32", 128, 128), ID, 0.5, ALU.mult)
+    for name, ds in (("shm", range(15, 7, -1)), ("trm", range(1, 8))):
+        for i, d in enumerate(ds):
+            ts(R(name, i * 128, 128), EE, float(d), ALU.is_equal)
+        m = R(name, 0, 128 * len(ds))
+        pick(m, m, [[0, len(ds)]] + DIAG, 0, -1.0)
+    ts(KM, R("ia"), 0.0, ALU.is_equal)
+    pick(MS, KM, DIAG, 0, 33.0)
+    ts(MN, BO, 2.0, ALU.mult)
+    pick(MN, MN, DIAG, 0, -62.0)
+    BOM = {16: BO}
+    for m in sorted(set(MOVED) - {0, 16}):
+        BOM[m] = CM(12 + len(BOM))
+        pick(BOM[m], BO, [[0, 32], [1, 4]], m // 4 - 4, 0.0, mult=0, keep=ALU.is_ge)
+    ts(QF, R("thi", 0, 1), -1.0, ALU.mult, 0.5, ALU.add)
+    ts(NB, R("thi", 1, 1), -1.0, ALU.mult, 0.5, ALU.add)
+    lent = [0]
 
-    ts(RHO, AG, -1.0, ALU.mult, 4.0, ALU.add)
+    def bank():
+        lent[0] += 1
+        return "~%d" % lent[0]
+
+    def weights(t, h):
+        lin(HB(h, 1), [(ID, half(R1, h)), (I3, half(NL[t % 2], h)), (ID, half(ONES, h))])
+        tt(half(WGT, h), half(WW, h), HB(h, 1), ALU.mult)
+
+    def spread(t, h):
+        if h not in BYDMA[t]:
+            return
+        tag[0], tag[2] = "wd", h
+        d, wd, ws = R(bank(), 0, H), "wd%d%d" % (t % 2, h), R("ws%d" % (t % 2), h * 2048, 2048)
+        w, wa, wb = half(WGT, h), half(WT[0], h), half(WT[1], h)
+        mm([(B(d[0])[:, 32 * b + 16 * c:32 * b + 16 * c + 16], T.bw[:, (2 * c + y) * 128:(2 * c + y + 1) * 128],
+             T.sb[:, w[1] + 2 * b + y:w[2]:8], y == 0, y == 1, 64) for b in range(4) for c in range(2) for y in range(2)],
+           [w, R("bw")], [d])
+        act(wa, d, ACT.Copy)
+        op("v", FIX + 64 * CY, [wa], [wb], lambda: g.vector.transpose(A(wb), A(wa)))
+        for i in range(2):
+            dma("s", T[wd][:, i, :], A(wb), [wb], [R(wd, i, 1)], ("wd%d%d" % (t, h), 16), lat=LAT_T)
+        for i in range(8):
+            dma("s", T[ws[0]][i:128:8, ws[1]:ws[2]], T[wd][:], [R(wd)], [ws], ("wi%d%d" % (t, h), 16), lat=LAT_W)
+            ops[-1]["adds"] = ("ws", t, h)
+
+    def gather(eng, out, tab, offs, c, extra):
+        o = R("off", offs * V + c * 64, 64)
+        if eng == "a":
+            fn = lambda: g.scalar.activation(A(out), T[tab][:, 0:WIN].indirect(A(o)), ACT.Copy)
+        else:
+            fn = lambda: g.vector.tensor_copy(A(out), T[tab][:, 0:WIN].indirect(A(o)))
+        op(eng, FIX + 1024 * GA * CY, [R(tab), o] + extra, [out], fn)
+        ops[-1]["ga"] = 1024
+
+    def jumps(offs, out, on_vector, h):
+        for c in (2 * h, 2 * h + 1):
+            gather("v" if c in on_vector else "a", R("jg", c * 1024, 1024), "jt", offs, c, [])
+        b, o = h * 2048, R(bank(), 0, H)
+        mm([(A(o), T.jd[:, k * 128:(k + 1) * 128], T.jg[:, b + k:b + 2048:16], k == 0, k == 15, H) for k in range(16)],
+           [R("jd"), R("jg", b, 2048)], [o])
+        act(half(out, h), o, ACT.Identity, bias=PKH)
+
+    def select(mask, val, h):
+        dh, dt, tmp = half(DH, h), half(DT, h), half(TMP, h)
+        tt(dt, half(val, h), dh, ALU.subtract)
+        tt(tmp, dt, half(mask, h), ALU.mult)
+        tt(dh, dh, tmp, ALU.add)
+
+    ts(R1, AG, -1.0, ALU.mult, 3.0, ALU.add)
     ts(NL[0], AG, 3.0, ALU.is_ge)
-    ts(I3, ID, 3.0, ALU.mult)
-    lin(R("pc", V, V), [(ID, RHO), (I3, NL[0])])
-    tt(WGT, WW, R("pc", V, V), ALU.mult)
-    cp(OFF(2), R("si"))
+    for h in range(2):
+        weights(0, h)
+    tag[0] = "init"
+    cp(OFF(STEPS), R("si"))
     tt(DT, R("si"), R("cr"), ALU.subtract)
     tt(TMP, DT, NL[0], ALU.mult)
     ts(DH, DT, 0.5, ALU.mult)
     tt(R("ci"), TMP, R("cr"), ALU.add)
     cp(OFF(0), R("ci"))
+    for h in range(2):
+        tag[0], tag[2] = "j", h
+        jumps(STEPS, JJ0, JV[0], h)
 
-    for k in range(16):
-        ts(R("jd", k * 128, 128), ID, MK(k), ALU.mult, 8.0, ALU.mult)
-    ts(R("i32", 0, 128), ID, 2.0 ** -11, ALU.mult)
-    ts(R("i32", 128, 128), ID, 0.5, ALU.mult)
-    for m, x in ((I241, 241.0), (IM15, -1.5), (IM3, -3.0), (IM1, -1.0), (I2, 2.0)):
-        act(m, ID, ACT.Copy, scale=x)
-    for name, ds, pb in (("shm", (15, 14, 13, 12), "pw0"), ("shm", (11, 10, 9, 8), "pw1"),
-                         ("trm", (1, 2, 3, 4), "pw2"), ("trm", (5, 6, 7), "px")):
-        c0 = 0 if ds[0] in (15, 1) else 512
-        for i, d in enumerate(ds):
-            m = R(name, c0 + i * 128, 128)
-            ts(m, EE, float(d), ALU.is_equal)
-            lin(R(pb, i * 128, 128), [(ID, m), (IM1, ID)])
-        act(R(name, c0, 128 * len(ds)), R(pb, 0, 128 * len(ds)), ACT.Copy)
-    ts(KM, R("ia"), 0.0, ALU.is_equal)
-    ts(MS, ID, 32.0, ALU.mult)
-    ts(MN, ID, -64.0, ALU.mult)
-    tt(MS, MS, KM, ALU.add)
-    tt(MN, MN, BO, ALU.add)
-    tt(MN, MN, BO, ALU.add)
-    act(I16TH, ID, ACT.Copy, scale=1.0 / 16)
-    act(R("gneg"), R("gsel"), ACT.Copy, scale=-1.0)
-    BOM = {}
-    for m in sorted(set(MOVED) - {0}):
-        BOM[m] = CM(12 + len(BOM))
-        ts(BOM[m], R("ik"), float(16 - m), ALU.is_ge)
-        tt(BOM[m], BOM[m], BO, ALU.mult)
-    op("v", FIX + 512 * CY, [], [R("seg")], lambda: g.vector.memset(T.seg[:], 1.0))
-    op("v", FIX + 64 * CY, [], [R("seg")], lambda: g.vector.memset(T.seg[:, 0:1024:16], 0.0))
-    ts(QF, R("thi", 0, 1), -1.0, ALU.mult, 0.5, ALU.add)
-    ts(NB, R("thi", 1, 1), -1.0, ALU.mult, 0.5, ALU.add)
-
-    def gather_act(out_ap, out_reg, tab, offs, c, extra):
-        o = R("off", offs * V + c * 64, 64)
-        op("a", FIX + 1024 * GA * CY, [R(tab), o] + extra, [out_reg],
-           lambda: g.scalar.activation(out_ap, T[tab][:, 0:WIN].indirect(A(o)), ACT.Copy))
-        ops[-1]["ga"] = 1024
-
-    def jumps(offs, out):
-        for c in range(4):
-            b = (c % 2) * 1024
-            gather_act(T.jg[:, b:b + 1024], R("jg", b, 1024), "jt", offs, c, [])
-            o = R("pr", V + c * 64, 64)
-            mm([(A(o), T.jd[:, k * 128:(k + 1) * 128], T.jg[:, b + k:b + 1024:16], k == 0, k == 15, 64) for k in range(16)],
-               [R("jd"), R("jg", b, 1024)], [o])
-        act(out, R("pr", V, V), ACT.Identity, bias=PKH)
-
-    def select(mask, val):
-        tt(DT, val, DH, ALU.subtract)
-        tt(TMP, DT, mask, ALU.mult)
-        tt(DH, DH, TMP, ALU.add)
-
-    jumps(2, JJ0)
-    select(NL[0], JJ0)
-    rot = [0]
-
-    def bank():
-        rot[0] += 1
-        return ("pw0", "pw1", "pw2", "px")[rot[0] % 4]
-
-    for t in range(STEPS):
-        p, last = t % 2, t == STEPS - 1
-        tx, tu, ws = "tx%d" % p, "tu%d" % p, "ws%d" % p
-        X, U, nl = XO(t), UO(t), NL[p]
-        tag[1], tag[0] = t, "xc"
-        lin(DT, [(ID, X)])
-        for c in range(4):
-            v0 = c * 64
-            tag[0] = "xc"
-            gather_act(T.xc[:, c * 1024:(c + 1) * 1024], R("xc", c * 1024, 1024), tx, p, c, [R("arrx", t, 1)])
-            for h in range(2):
-                b, v1 = bank(), v0 + 32 * h
+    def activity(t, h):
+        tx, ws, hb = table("x", t), "ws%d" % (t % 2), bank()
+        tag[2] = h
+        tag[0] = "xc"
+        for c in (2 * h, 2 * h + 1):
+            gather("v" if c in XV[t] else "a", R("xc", c * 1024, 1024), tx, t, c, [R("arrx", t, 1), R("arry", t, 1)])
+        n = 128 if h in WIDE else 64
+        s, m = n // 32, 512 // n
+        for v0 in range(h * H, h * H + H, n):
+            c0 = 16 * v0
+            for e in range(s):
+                b, o = bank(), R("wx", c0 + e * 512, 512)
                 tag[0] = "xw"
-                mm([(T[b][:, k:512:16], T.selw[:, k * 128:(k + 1) * 128], T.sb[:, WGT[1] + v1:WGT[1] + v1 + 32],
-                     True, True, 64) for k in range(16)], [R("selw"), WGT], [R(b)])
-                tt(R("wx", (c % 2) * 1024 + h * 512, 512), R("xc", 16 * v1, 512), R(b), ALU.mult)
-                tag[0] = "ws"
-                act(R(ws, 16 * v1, 512), R(b), ACT.Copy)
+                sel = [R("selw", (k % 2 * 8 + k // 2) * 128, 128) for k in range(e, 16, s)]
+                mm([(B(b)[:, i:512:m], A(sel[i]), T.sb[:, WGT[1] + v0:WGT[1] + v0 + n], True, True, n) for i in range(m)],
+                   sel + [half(WGT, h)], [R(b, 0, 512)])
+                op("v", FIX + 512 * CY, [R("xc", c0, 16 * n), R(b, 0, 512)], [o],
+                   lambda o=o, b=b, c0=c0, e=e: g.vector.tensor_tensor(A(o), T.xc[:, c0 + e:c0 + 16 * n:s], B(b)[:], ALU.mult))
+                if h not in BYDMA[t]:
+                    tag[0] = "ws"
+                    op("a", FIX + 512 * CY, [R(b, 0, 512)], [R(ws, c0, 16 * n)],
+                       lambda b=b, c0=c0, e=e: g.scalar.activation(T[ws][:, c0 + e:c0 + 16 * n:s], B(b)[:], ACT.Copy),
+                       adds=("ws", t, v0))
             tag[0] = "xw"
-            o = R("ph", v0, 64)
-            b0 = (c % 2) * 1024
-            mm([(A(o), T.i16[:], T.wx[:, b0 + k:b0 + 1024:16], k == 0, k == 15, 64) for k in range(16)],
-               [R("i16"), R("wx", b0, 1024)], [o])
+            o = R(hb, v0 - h * H, n)
+            for k0 in range(0, 16, 1024 // n):
+                mm([(A(o), T.i16[:], T.wx[:, c0 + k // m * 512 + k % m:c0 + k // m * 512 + 512:m], k == 0, k == 15, n)
+                    for k in range(k0, k0 + 1024 // n)], [R("i16"), R("wx", c0 + k0 * n, 1024)], [o])
         tag[0] = "nx"
-        ts(XB, R("ph", 0, V), 15.0, ALU.min, 128.501953125, ALU.add)
-        XN = XO(t + 1)
-        ts(XN, XB, -129.0, ALU.add)
-        if not last:
-            send("x", t + 1)
+        xn, e = half(XO(t + 1), h), R(bank(), 0, H)
+        ts(half(XB, h), R(hb, 0, H), 15.0, ALU.min, 128.501953125, ALU.add)
+        if XNA:
+            act(xn, half(XB, h), ACT.Identity, bias=COL(32))
         else:
-            act(OX, XN, ACT.Copy)
-            dma("s", T.yx[:], A(OX), [OX], [], ("out", 16))
-        lin(R("ph", V, V), [(BO, XN)])
-        act(SS, R("ph", V, V), ACT.Sign, bias=NB)
-        C = R("pc", 0, V)
-        tag[0] = "mn"
-        mv = MOVED[t]
-        lin(C, [(I241, nl)] + ([(BOM[mv], X)] if mv else []), stop=False)
-        turn = list(range(16 - mv))
-        for i in range(mv):
-            turn.insert(i * 16 // mv, 16 - mv + i)
-        for i, k in enumerate(turn):
-            o = R("mn", i * V, V)
-            if k < 16 - mv:
-                w = V // 2 if k < HALF else V
-                for v0 in range(0, V, w):
-                    o2, x2 = R("mn", i * V + v0, w), R("pd", V + v0, w)
-                    op("v", FIX + w * CY, [R("xc", 16 * v0, 16 * w), x2], [o2],
-                       lambda o2=o2, x2=x2, k=k, v0=v0, w=w: g.vector.tensor_tensor(
-                           A(o2), T.xc[:, 16 * v0 + k:16 * (v0 + w):16], A(x2), ALU.min))
-                lin(C, [(R("gsel", 15 - k, 128), o)], start=False, stop=i == 15)
+            ts(xn, half(XB, h), -129.0, ALU.add)
+        lin(e, [(BO, xn)])
+        act(half(SS, h), e, ACT.Sign, bias=NB)
+        if t == STEPS - 1:
+            act(half(OX, h), xn, ACT.Copy)
+            dma("s", T.yx[:, h * H:h * H + H], A(half(OX, h)), [half(OX, h)], [], ("out", 16))
+
+    def tags(t, h):
+        last, mv, c0 = t == STEPS - 1, MOVED[t], h * 2048
+        x, nl, dt, dh = half(XO(t), h), half(NL[t % 2], h), half(DT, h), half(DH, h)
+        key, fresh, cap, r1, ww = [half(y, h) for y in (KEY, FRESH, CAP, R1, WW)]
+        ci, cr = half(R("ci"), h), half(R("cr"), h)
+        C, Z = HB(h, 0), HB(h, 1)
+        tag[0], tag[2] = "mn", h
+        lin(C, [(I241, nl)], stop=False)
+        if mv < 16:
+            x4 = R(bank(), 0, 512)
+            mm([(B(x4[0])[:, i:512:4], A(ID), A(x), True, True, H) for i in range(4)], [ID, x], [x4])
+        for j in range(4):
+            o = R("mn", c0 + j * 512, 512)
+            if j < 4 - mv // 4:
+                op("v", FIX + 512 * CY, [R("xc", c0, 2048), x4], [o],
+                   lambda j=j, o=o: g.vector.tensor_tensor(A(o), T.xc[:, c0 + j:c0 + 2048:4], A(x4), ALU.min))
+                sign = "gsel"
             else:
-                d = R(bank(), 0, V)
-                mm([(A(d), A(ID), A(X), True, False, V), (A(d), A(IM1), T.xc[:, k:16 * V:16], False, True, V)],
-                   [ID, IM1, X, R("xc")], [d])
-                act(o, d, ACT.Relu)
-                lin(C, [(R("gneg", 15 - k, 128), o)], start=False, stop=i == 15)
+                b, sign = bank(), "gneg"
+                mm([(B(b)[:], A(IM1), T.xc[:, c0 + j:c0 + 2048:4], True, False, 512)]
+                   + [(B(b)[:, i:512:4], A(ID), A(x), False, i == 3, H) for i in range(4)],
+                   [ID, IM1, x, R("xc", c0, 2048)], [R(b, 0, 512)])
+                act(o, R(b, 0, 512), ACT.Relu)
+            end = j == 3 and not mv
+            mm([(A(C), T[sign][:, 15 - j - 4 * i:143 - j - 4 * i], T.mn[:, o[1] + i:o[2]:4], False, end and i == 3, H)
+                for i in range(4)], [R(sign), o], [C], adds=None if end else (C, t))
+        if mv:
+            lin(C, [(BOM[mv], x)], start=False)
         tag[0] = "tail"
-        act(KEY, C, ACT.Identity, bias=R("col", 4, 1))
-        act(FRESH, KEY, ACT.Sign, bias=QF)
-        Z = R("pc", V, V)
-        first = True
-        for d2 in range(4):
-            b = bank()
-            for i in range(2):
-                d = 2 * d2 + i + 1
-                lin(R(b, i * V, V), [(R("shm", (d - 1) * 128, 128), KEY)])
-            for i in range(2):
-                d = 2 * d2 + i + 1
-                act(R("sg", (d - 1) * V, V), R(b, i * V, V), ACT.Sign, bias=TB(d))
-            terms = [(R("trm", (d - 1) * 128, 128) if d < 8 else IM1, R("sg", (d - 1) * V, V)) for d in (2 * d2 + 1, 2 * d2 + 2)]
-            if first:
-                terms = [(MN, nl), (MS, SS)] + terms
-            lin(Z, terms, start=first, stop=d2 == 3)
-            first = False
-        act(cap, Z, ACT.Sign, bias=R("col", 7, 1))
+        act(key, C, ACT.Identity, bias=COL(4))
+        act(fresh, key, ACT.Sign, bias=QF)
+        lin(Z, [(MN, nl)], stop=False)
+        sg = lambda d: R("sg", h * 1024 + (d - 1) * H, H)
+        for d4 in range(2):
+            b, ds = bank(), range(4 * d4 + 1, 4 * d4 + 5)
+            mm([(B(b)[:, (d - ds[0]) * H:(d - ds[0] + 1) * H], T.shm[:, (d - 1) * 128:d * 128], A(key), True, True, H)
+                for d in ds], [R("shm"), key], [R(b, 0, 512)])
+            for d in ds:
+                act(sg(d), R(b, (d - ds[0]) * H, H), ACT.Sign, bias=TB(d))
+            for d in ds[::2]:
+                lin(Z, [(R("trm", (j - 1) * 128, 128) if j < 8 else IM1, sg(j)) for j in (d, d + 1)], start=False, stop=False)
+        lin(Z, [(MS, half(SS, h))], start=False)
+        act(cap, Z, ACT.Sign, bias=COL(7))
+        tag[0] = "j"
+        if t == 0:
+            select(NL[0], JJ0, h)
         if t in (1, 3):
-            tag[0] = "j"
-            ts(CAP1, cap, 0.0, ALU.is_gt)
-            jumps(p, JJC)
-            select(nl, JJC)
-        tag[0] = "l"
+            act(half(CAP1, h), cap, ACT.Relu)
+            jumps(t, JJC, JV[(t + 1) // 2], h)
+            select(NL[t % 2], JJC, h)
         if t == 1:
-            ts(L2, RHO, 2.0, ALU.is_equal)
-        tag[0] = "m"
+            ts(half(L2, h), r1, 1.0, ALU.is_equal)
         if t == 2:
-            select(L2, JJ0)
-        tag[0] = "s"
+            select(L2, JJ0, h)
         if t in (2, 4):
-            select(CAP1, JJC)
+            select(CAP1, JJC, h)
         tag[0] = "end"
-        tt(CPRE, R("ci"), DH, ALU.add)
-        lin(R("ph", 0, V), [(IM1, RHO), (IM3, nl), (ID, FRESH)], stop=False)
-        lin(R("ph", 0, V), [(IM1, cap)], start=False)
-        act(SW2, R("ph", 0, V), ACT.Sign, bias=R("col", 5, 1), scale=-1.0)
-        tt(DH, DH, SW2, ALU.mult)
-        tt(R("cr"), CPRE, DH, ALU.subtract)
-        ts(R("ci"), R("cr"), WIN - 1, ALU.bitwise_and)
+        tt(half(CPRE, h), ci, dh, ALU.add)
+        lin(HB(h, 2), [(IM1, r1), (IM3, nl), (ID, fresh), (IM1, cap)])
+        act(half(SW2, h), HB(h, 2), ACT.Sign, bias=COL(5), scale=-1.0)
+        tt(dh, dh, half(SW2, h), ALU.mult)
+        tt(cr, half(CPRE, h), dh, ALU.subtract)
+        ts(ci, cr, WIN - 1, ALU.bitwise_and)
         if not last:
-            cp(OFF(1 - p), R("ci"))
+            cp(half(OFF(t + 1), h), ci)
         else:
-            cp(OC, R("ci"))
-            dma("s", T.yc[:], A(OC), [OC], [], ("out", 16))
-        lin(R("ph", V, V), [(ID, RHO), (I2, FRESH), (IM15, cap)])
-        ts(RHO, R("ph", V, V), -0.5, ALU.add, 1.0, ALU.max)
-        lin(R("pc", 0, V), [(ID, WW), (I2, cap)])
-        ts(WW, R("pc", 0, V), 2.0, ALU.add, 15.0, ALU.min)
+            cp(half(OC, h), ci)
+            dma("s", T.yc[:, h * H:h * H + H], A(half(OC, h)), [half(OC, h)], [], ("out", 16))
+        lin(HB(h, 3), [(ID, r1), (I2, fresh), (IM15, cap)])
+        act(r1, HB(h, 3), ACT.Relu, bias=COL(6))
+        lin(C, [(ID, ww), (I2, cap)])
+        ts(ww, C, 2.0, ALU.add, 15.0, ALU.min)
         if not last:
-            ts(NL[1 - p], RHO, 2.0, ALU.is_lt)
-            lin(R("pc", V, V), [(ID, RHO), (I3, NL[1 - p])])
-            tt(WGT, WW, R("pc", V, V), ALU.mult)
+            if NLA:
+                act(half(NL[1 - t % 2], h), r1, ACT.Relu, bias=R("sb", ONES[1], 1), scale=-1.0)
+            else:
+                ts(half(NL[1 - t % 2], h), r1, 1.0, ALU.is_lt)
+            weights(t + 1, h)
         else:
-            ts(DT, RHO, -16.0, ALU.mult, 64.0, ALU.add)
-            tt(JJ0, DT, WW, ALU.add)
-            dma("s", T.yw[:], A(JJ0), [JJ0], [], ("out", 16))
+            ts(dt, r1, -16.0, ALU.mult, 48.0, ALU.add)
+            tt(half(JJ0, h), dt, ww, ALU.add)
+            dma("s", T.yw[:, h * H:h * H + H], A(half(JJ0, h)), [half(JJ0, h)], [], ("out", 16))
+
+    def potentials(t):
+        tx, tu, ws = table("x", t), table("u", t), "ws%d" % (t % 2)
         tag[0] = "u"
         for c in range(4):
-            v0, b0 = c * 64, (c % 2) * 1024
-            for h in range(2):
-                v1, b1 = v0 + 32 * h, b0 + 512 * h
-                o = R("off", p * V + v1, 32)
-                op("v", FIX + 512 * GA * CY, [R(tu), o, R(ws, 16 * v1, 512), R("arru", t, 1), R("arrv", t, 1)], [R("wu", b1, 512)],
-                   lambda o=o, b1=b1, v1=v1, tu=tu, ws=ws: g.vector.tensor_tensor(
-                       T.wu[:, b1:b1 + 512], T[tu][:, 0:WIN].indirect(A(o)), T[ws][:, 16 * v1:16 * v1 + 512], ALU.mult))
-                ops[-1]["ga"] = 512
-            r = R("pr", v0, 64)
-            items = ([(A(r), A(I16TH), T[tx][:, q * V + v0:q * V + v0 + 64], True, False, 64),
-                      (A(r), T.i32[:, 128:256], T[tu][:, q * V + v0:q * V + v0 + 64], False, False, 256)]
+            v0, b0, s0 = c * 64, c * 1024, (c % 2) * 1024
+            tag[2] = c // 2
+            for b1 in range(b0, b0 + 1024, UW):
+                o = R("off", t * V + b1 // 16, UW // 16)
+                op("v", FIX + UW * GA * CY, [R(tu), o, R(ws, b0, 1024), R("arru", t, 1), R("arrv", t, 1)], [R("wu", b1, UW)],
+                   lambda o=o, b1=b1: g.vector.tensor_tensor(
+                       T.wu[:, b1:b1 + UW], T[tu][:, 0:WIN].indirect(A(o)), T[ws][:, b1:b1 + UW], ALU.mult))
+                ops[-1]["ga"] = UW
+            r, x, u = R("pr", v0, 64), R(tx, q * V + v0, 64), R(tu, q * V + v0, 64)
+            items = ([(A(r), A(I16TH), A(x), True, False, 64), (A(r), T.i32[:, 128:256], A(u), False, False, 256)]
                      + [(A(r), T.i32[:, 0:128], T.wu[:, b0 + k:b0 + 1024:16], False, k == 15, 256) for k in range(16)])
             if c in SCAN[t]:
-                op("v", FIX + 1024 * CY, [R("seg"), R("wu", b0, 1024)], [R("su")],
-                   lambda b0=b0: g.vector.tensor_tensor_scan(T.su[:], T.seg[:], T.wu[:, b0:b0 + 1024], 0.0, ALU.mult, ALU.add))
-                mm(items[:2] + [(A(r), T.i32[:, 0:128], T.su[:, 15:1024:16], False, True, 256)],
-                   [I16TH, R("i32"), X, U, R("su")], [r])
-            for i in range(0, 0 if c in SCAN[t] else 18, 3):
-                mm(items[i:i + 3], [I16TH, R("i32"), X, U, R("wu", b0, 1024)], [r])
+                op("v", FIX + 1024 * CY, [R("seg"), R("wu", b0, 1024)], [R("su", s0, 1024)],
+                   lambda b0=b0, s0=s0: g.vector.tensor_tensor_scan(
+                       T.su[:, s0:s0 + 1024], T.seg[:], T.wu[:, b0:b0 + 1024], 0.0, ALU.mult, ALU.add))
+                mm(items[:2] + [(A(r), T.i32[:, 0:128], T.su[:, s0 + 15:s0 + 1024:16], False, True, 256)],
+                   [I16TH, R("i32"), x, u, R("su", s0, 1024)], [r])
+            for i in range(0, 0 if c in SCAN[t] else 18, 2):
+                mm(items[i:i + 2], [I16TH, R("i32"), x, u, R("wu", b0, 1024)], [r])
             if c % 2:
-                c0 = v0 - 64
-                un = R(UO(t + 1)[0], q * V + c0, 128)
-                act(un, R("pr", c0, 128), ACT.Tanh, bias=R("col", 6, 1))
-                if not last:
+                un = half(UO(t + 1), c // 2)
+                act(un, R("pr", v0 - 64, H), ACT.Tanh, bias=COL(6))
+                if t < STEPS - 1:
                     send("uv"[c // 2], t + 1)
                 else:
-                    dma("s", T.yu[:, c0:c0 + 128], A(un), [un], [], ("out", 16))
+                    dma("s", T.yu[:, v0 - 64:v0 + 64], A(un), [un], [], ("out", 16))
 
-    head = []
-    for i, x in ((4, -241.0), (5, -2.5), (6, -0.5), (7, -39.5)):
-        head.append({"eng": "v", "cost": 110.0, "r": [], "w": [COL(i)], "sem": None, "lat": 0.0, "tag": "init", "step": -1,
-                     "fn": lambda i=i, x=x: g.vector.memset(A(COL(i)), x)})
-    return head + ops
+    for t in range(STEPS):
+        tag[1] = t
+        for h in range(2):
+            spread(t, h)
+            activity(t, h)
+            if t < STEPS - 1 and (XH or h):
+                send("xy"[h] if XH else "x", t + 1)
+        tags(t, 0)
+        tags(t, 1)
+        potentials(t)
+    return ops
+
+
+def in_turn(a, b):
+    return a["eng"] == b["eng"] == "t" or (a["remote"] and a["remote"] == b["remote"])
 
 
 def meet(a, b):
@@ -475,103 +561,171 @@ def depend(ops):
     seen = {}
     for i, o in enumerate(ops):
         for reg, wr in [(x, False) for x in o["r"]] + [(x, True) for x in o["w"]]:
+            bank = wr and o["eng"] == "t" and reg[0] in ("pc", "ph", "pr")
             for j, reg2, wr2 in seen.get(reg[0], []):
-                if j != i and (wr or wr2) and meet(reg, reg2):
-                    deps[i].add(j)
-            if wr and o["eng"] == "t" and reg[0] in ("pc", "ph", "pr"):
-                deps[i].update(j for j, reg2, wr2 in seen.get(reg[0], []) if j != i and wr2)
+                if j != i and ((wr or wr2) and meet(reg, reg2) or bank and wr2):
+                    if not (o["adds"] and o["adds"] == ops[j]["adds"]):
+                        deps[i].add(j)
         for reg, wr in [(x, False) for x in o["r"]] + [(x, True) for x in o["w"]]:
             seen.setdefault(reg[0], []).append((i, reg, wr))
     return deps
 
 
-def place(ops, pred, rank, back):
-    start, busy = {}, {}
-    for i in sorted(range(len(ops)), key=lambda i: rank[i]):
-        o, s = ops[i], 0.0
-        e, c = o["eng"], o["cost"]
-        for j in pred[i]:
-            f = ops[j]["eng"]
-            gap = SYNC if f != e else 0.0 if e == "t" else 60.0
-            lat = 0.0 if e == f == "g" else o["lat"] if back else ops[j]["lat"]
-            s = max(s, start[j] + ops[j]["cost"] + lat + gap)
-        if back and not pred[i]:
-            s = o["lat"]
-        res = ([e] if e else []) + o["banks"]
-        again = True
-        while again:
-            again = False
-            for r in res:
-                lst = busy.setdefault(r, [])
-                lo, hi = 0, len(lst)
-                while lo < hi:
-                    mid = (lo + hi) // 2
-                    if lst[mid][1] + SYNC <= s:
-                        lo = mid + 1
-                    else:
-                        hi = mid
-                for a, b, f in lst[lo:]:
-                    m = 0.0 if f == e else SYNC
-                    if a - m >= s + c:
-                        break
-                    if b + m > s:
-                        s, again = b + m, True
-        start[i] = s
-        for r in res:
-            busy[r].append((s, s + c, e))
-            busy[r].sort()
-    return [start[i] for i in range(len(ops))]
-
-
-def times(ops, deps, succ, seed):
+def lay(ops, pred, succ, uses, rank, first, before):
     n = len(ops)
-    level = [0.0] * n
-    for i in range(n - 1, -1, -1):
-        level[i] = ops[i]["cost"] + ops[i]["lat"] + 1.0 + max([level[j] for j in succ[i]] + [0.0])
-    rank, best = [-x for x in level], None
-    for turn in range(TURNS):
-        at = place(ops, deps, rank, False)
-        end = max(at[i] + ops[i]["cost"] + ops[i]["lat"] for i in range(n))
-        if best is None or end < best[0]:
-            best = (end, at)
-        rank = [0.0] * n
-        for i in range(n - 1, -1, -1):
-            seed = (seed * 1103515245 + 12345) % 2147483648
-            rank[i] = max([-at[i] - ops[i]["cost"] + (seed % 1000) * JITTER] + [rank[j] + 0.001 for j in succ[i]])
-        bt = place(ops, succ, rank, True)
-        rank = [0.0] * n
-        for i in range(n):
-            rank[i] = max([-bt[i] - ops[i]["cost"]] + [rank[j] + 0.001 for j in deps[i]])
-    return best[1]
+    left = [len(d) for d in pred]
+    at, end, ready = [0.0] * n, [0.0] * n, {}
+    free, touched, banks, order = {e: 0.0 for e in ("v", "a", "t", "g", "s", None)}, {}, {}, []
+    holder = {b: None for b in LENT}
+    todo = {x: len(uses[x]) for x in uses}
+    back = {b: -SYNC for b in LENT}
+    eng = [o["eng"] for o in ops]
+    cost = [o["cost"] for o in ops]
+    for i in range(n):
+        if not left[i]:
+            ready[i] = first[i]
+    done = [False] * n
+    while ready:
+        c, who, est = 1e18, None, {}
+        idle = [back[x] for x in LENT if holder[x] is None]
+        for i, s in ready.items():
+            e = eng[i]
+            if free[e] > s:
+                s = free[e]
+            for b in ops[i]["banks"]:
+                if b in touched:
+                    for f, x in touched[b].items():
+                        if f != e and x + SYNC > s:
+                            s = x + SYNC
+                elif b[0] == "~":
+                    if not idle or not all(done[j] for j, x in before[b]):
+                        s = None
+                        break
+                    s = max([s, min(idle) + SYNC] + [end[j] + x - cost[i] - EARLY for j, x in before[b]])
+            if s is not None:
+                est[i] = s
+                if s + cost[i] < c:
+                    c, who = s + cost[i], i
+        if who is None:
+            return None
+        i, e = who, eng[who]
+        if e:
+            i = min((j for j in est if eng[j] == e and est[j] < c), key=lambda j: rank[j] + HASTE * est[j])
+        s = est[i]
+        at[i], end[i] = s, s + cost[i]
+        done[i] = True
+        if e:
+            free[e] = end[i]
+        for b in ops[i]["banks"]:
+            if b[0] == "~":
+                if b not in banks:
+                    x = max((x for x in LENT if holder[x] is None and back[x] + SYNC <= s + 1e-6), key=lambda x: back[x])
+                    banks[b], holder[x] = x, b
+                todo[b] -= 1
+                back[banks[b]] = max(back[banks[b]], end[i])
+                if not todo[b]:
+                    holder[banks[b]] = None
+            touched.setdefault(b, {})[e] = end[i]
+        order.append(i)
+        del ready[i]
+        for j, x in succ[i]:
+            left[j] -= 1
+            if not left[j]:
+                ready[j] = max([first[j]] + [end[k] + y for k, y in pred[j]])
+    return order, banks, at, end
 
 
 def schedule(ops, seed):
     n = len(ops)
     deps = depend(ops)
-    succ = [[] for _ in range(n)]
+    uses, pred, succ = {}, [[] for _ in range(n)], [[] for _ in range(n)]
     for i in range(n):
-        ops[i]["banks"] = sorted(set(x[0] for x in ops[i]["r"] + ops[i]["w"] if x[0] in PSUM))
-        for j in deps[i]:
-            succ[j].append(i)
-    key = times(ops, deps, succ, seed)
-    for i in range(n):
-        ops[i]["at"] = key[i]
-    left = [len(d) for d in deps]
-    ready = [i for i in range(n) if left[i] == 0]
-    used, order = {}, []
-    while ready:
-        i = min(ready, key=lambda i: (key[i], i))
+        ops[i]["banks"] = sorted(set(x[0] for x in ops[i]["r"] + ops[i]["w"] if x[0] in PSUM or x[0][0] == "~"))
+        for b in ops[i]["banks"]:
+            if b[0] == "~":
+                uses.setdefault(b, []).append(i)
         e = ops[i]["eng"]
-        for b in set(x[0] for x in ops[i]["r"] + ops[i]["w"] if x[0] in PSUM):
+        for j in sorted(deps[i]):
+            f = ops[j]["eng"]
+            x = (SYNC if f != e else 0.0 if e == "t" else 60.0) + (0.0 if in_turn(ops[i], ops[j]) else ops[j]["lat"])
+            pred[i].append((j, x))
+            succ[j].append((i, x))
+    on = {}
+    for i, o in enumerate(ops):
+        on.setdefault((o["eng"], o["tag"], o["step"], o["half"]), []).append(i)
+    for t in range(STEPS):
+        for e, first, then, dt in FENCES:
+            for a in [i for x in first.split() for i in on.get((e, x[:-1], t, int(x[-1])), [])]:
+                for b in [i for x in then.split() for i in on.get((e, x[:-1], t + dt, int(x[-1])), [])]:
+                    pred[b].append((a, 0.0))
+                    succ[a].append((b, 0.0))
+    left = [len(x) for x in pred]
+    turn = [i for i in range(n) if not left[i]]
+    for i in turn:
+        for j, x in succ[i]:
+            left[j] -= 1
+            if not left[j]:
+                turn.append(j)
+    fore, aft, safe = {}, {}, {}
+    for b in uses:
+        reader = [i for i in uses[b] if ops[i]["eng"] != "t"][0]
+        fore[b] = [(j, x) for j, x in pred[reader] if j not in uses[b]]
+        safe[b] = fore[b] + [(j, -1e9) for i in uses[b] for j, x in pred[i] if j not in uses[b]]
+        aft[b] = [(j, -1e9) for i in uses[b] for j, x in succ[i] if j not in uses[b]]
+    lat, zero, level = [o["lat"] for o in ops], [0.0] * n, [0.0] * n
+    kind = [(o["tag"], o["step"], o["half"]) for o in ops]
+    for i in reversed(turn):
+        level[i] = ops[i]["cost"] + max([lat[i]] + [level[j] + x for j, x in succ[i]])
+    top, kinds, state = {}, sorted(set(kind)), [seed]
+    for i in range(n):
+        top[kind[i]] = max(top.get(kind[i], 0.0), level[i])
+
+    def chance():
+        state[0] = (state[0] * 1103515245 + 12345) % 2147483648
+        return (state[0] >> 8) / 8388608.0
+
+    def span(got):
+        order, banks = got[0], got[1]
+        end, free, used = [0.0] * n, {}, {}
+        for i in order:
+            e = ops[i]["eng"]
+            s = max([free.get(e, 0.0)] + [end[j] + x + late[j] for j, x in pred[i]])
+            for b in ops[i]["banks"]:
+                for f, x in used.setdefault(banks.get(b, b), {}).items():
+                    if f != e and x + SYNC > s:
+                        s = x + SYNC
+            end[i] = s + ops[i]["cost"] * (SLOW if e == "t" else 1.0)
+            for b in ops[i]["banks"]:
+                used[banks.get(b, b)][e] = end[i]
+            if e:
+                free[e] = end[i]
+        return max(got[3][i] + lat[i] for i in range(n)) + CARE * max(end)
+    late = [LATE if o["eng"] is None else 0.5 * o["lat"] if o["eng"] == "s" else 0.0 for o in ops]
+    rank = [-1e5 - level[i] if kind[i][0] == "init" else
+            1000.0 * (PERIOD * max(0, kind[i][1]) + PHASES[kind[i][0]][kind[i][2]]) + 0.1 * (top[kind[i]] - level[i])
+            for i in range(n)]
+    now = lay(ops, pred, succ, uses, rank, zero, safe)
+    best = now = now + (span(now),)
+    for turn in range(TURNS):
+        shift = {kinds[int(chance() * len(kinds))]: (2 * chance() - 1) * JITTER for _ in range(1 + int(6 * chance()))}
+        rank = [shift.get(kind[i], 0.0) - now[3][i] for i in range(n)]
+        got = lay(ops, succ, pred, uses, rank, lat, {b: [] for b in uses}) or lay(ops, succ, pred, uses, rank, lat, aft)
+        rank = [-got[3][i] - URGE * lat[i] - RUSH.get(kind[i][::2], 0.0) for i in range(n)]
+        got = lay(ops, pred, succ, uses, rank, zero, fore) or lay(ops, pred, succ, uses, rank, zero, safe)
+        got += (span(got),)
+        if got[4] <= now[4] + DRIFT * chance():
+            now = got
+            if now[4] < best[4]:
+                best = now
+    order, banks = best[0], best[1]
+    used = {}
+    for i in order:
+        e = ops[i]["eng"]
+        for b in ops[i]["banks"]:
+            b = banks.get(b, b)
             deps[i].update(j for e2, j in used.get(b, {}).items() if e2 != e)
             used.setdefault(b, {})[e] = i
-        order.append(i)
-        ready.remove(i)
-        for j in succ[i]:
-            left[j] -= 1
-            if left[j] == 0:
-                ready.append(j)
-    return order, deps
+    return order, deps, banks
 
 
 PLAN = {}
@@ -583,21 +737,20 @@ def rank_program(g, core, T, topo):
             if T.rank_of(owner) is not None:
                 relay_program(g, core, T, topo, owner)
         return
-    ops = build(g, core, T, topo)
     if "order" not in PLAN:
-        PLAN["order"], PLAN["deps"] = schedule(ops, SEED)
+        PLAN["order"], PLAN["deps"], PLAN["banks"] = schedule(build(g, core, T, topo, {}), SEED)
     order, deps = PLAN["order"], PLAN["deps"]
+    ops = build(g, core, T, topo, PLAN["banks"])
     queue = {"v": g.vector, "a": g.scalar, "t": g.tensor, "g": g, "s": g.sync}
-    needed = set(j for i in order for j in deps[i] if ops[i]["eng"] is not None
-                 and not (ops[i]["eng"] == "t" and ops[j]["eng"] == "t"))
-    count, token, waited, total = {}, {}, {}, {}
+    needed = set(j for i in order for j in deps[i] if ops[i]["eng"] is not None and not in_turn(ops[i], ops[j]))
+    token, waited, total = {}, {}, {}
     for i in order:
         o = ops[i]
         e = o["eng"]
         if e is not None:
             want = {}
             for j in deps[i]:
-                if j in token and not (e == "t" and ops[j]["eng"] == "t"):
+                if j in token and not in_turn(o, ops[j]):
                     s, x = token[j]
                     want[s] = max(want.get(s, 0), x)
             for s in sorted(want):

from concourse.bass import DstId, RemoteDMATransfer
from concourse.mybir import AluOpType, ActivationFunctionType

ALU = AluOpType
ACT = ActivationFunctionType
STEPS, V, WIN = 5, 256, 2048
H = V // 2

SCRATCH = {
    "tx0": ("sbuf", [128, WIN], "bfloat16"), "tx1": ("sbuf", [128, WIN], "bfloat16"),
    "tx2": ("sbuf", [128, WIN], "bfloat16"),
    "tu0": ("sbuf", [128, WIN], "float32"), "tu1": ("sbuf", [128, WIN], "float32"),
    "wd00": ("dram", [8, 2, 16 * H], "bfloat16"), "wd01": ("dram", [8, 2, 16 * H], "bfloat16"),
    "wd10": ("dram", [8, 2, 16 * H], "bfloat16"), "wd11": ("dram", [8, 2, 16 * H], "bfloat16"),
    "jt": ("sbuf", [128, WIN], "bfloat16"),
    "xc": ("sbuf", [128, 16 * V], "bfloat16"),
    "ws0": ("sbuf", [128, 16 * V], "bfloat16"), "ws1": ("sbuf", [128, 16 * V], "bfloat16"),
    "wx": ("sbuf", [128, 4096], "float16"),
    "mn": ("sbuf", [128, 4096], "bfloat16"),
    "wu": ("sbuf", [128, 4096], "float32"),
    "jg": ("sbuf", [128, 4096], "bfloat16"),
    "sg": ("sbuf", [128, 2048], "bfloat16"),
    "zr": ("sbuf", [128, 1024], "bfloat16"),
    "selw": ("sbuf", [128, 2048], "bfloat16"), "jd": ("sbuf", [128, 2048], "bfloat16"),
    "shm": ("sbuf", [128, 1024], "bfloat16"), "trm": ("sbuf", [128, 1024], "bfloat16"),
    "cm": ("sbuf", [128, 128 * 18], "bfloat16"), "bw": ("sbuf", [128, 512], "bfloat16"),
    "gsel": ("sbuf", [128, 144], "bfloat16"), "gneg": ("sbuf", [128, 144], "bfloat16"),
    "seg": ("sbuf", [128, 1024], "bfloat16"), "su": ("sbuf", [128, 2048], "float32"),
    "i16": ("sbuf", [128, 128], "float16"),
    "i32": ("sbuf", [128, 256], "float32"),
    "ia": ("sbuf", [128, 128], "int32"), "ib": ("sbuf", [128, 128], "int32"), "ic": ("sbuf", [128, 144], "int32"),
    "ip": ("sbuf", [128, 16], "int32"),
    "col": ("sbuf", [128, 40], "float32"),
    "thi": ("sbuf", [128, 2], "int32"),
    "si": ("sbuf", [128, V], "int32"), "ci": ("sbuf", [128, V], "int32"), "cr": ("sbuf", [128, V], "int32"),
    "off": ("sbuf", [128, 6 * V], "uint16"),
    "sb": ("sbuf", [128, 17 * V], "bfloat16"),
    "sf": ("sbuf", [128, 6 * V], "float32"),
    "pw0": ("psum", [128, 512], "float32"), "pw1": ("psum", [128, 512], "float32"),
    "pw2": ("psum", [128, 512], "float32"), "ph": ("psum", [128, 512], "float32"),
    "pc": ("psum", [128, 512], "float32"), "pr": ("psum", [128, 512], "float32"),
    "pd": ("psum", [128, 512], "float32"), "px": ("psum", [128, 512], "float32"),
}
LOADS = ["x", "u", "a", "p", "s", "w", "t", "j"]
SEMAPHORES = (["qv", "qa", "qt", "qg", "out"] + ["ld" + n for n in LOADS]
              + [k + str(t) for k in ("xa", "ya", "ua", "va", "xl", "yl", "ul", "vl") for t in range(STEPS)]
              + ["%s%d%d" % (k, t, h) for k in ("wd", "wi") for t in range(STEPS) for h in range(2)])
PSUM = ("ph", "pc", "pr", "pd")
LENT = ("pw0", "pw1", "pw2", "px")

CY, PE, GA, FIX, SYNC = 0.83, 0.42, 1.5, 60.0, 120.0
LAT_X, LAT_U, LAT_DMA, LAT_T, LAT_W = 8000.0, 8500.0, 2200.0, 3000.0, 5000.0
TURNS, JITTER, SEED, HASTE, EARLY, DRIFT = 300, 1500.0, 3, 8.0, 200.0, 1000.0
RUSH = {}
FENCES = []
PERIOD, URGE, LATE, SLOW, CARE = 17.3, 10.0, 3000.0, 1.6, 0.3
PHASES = {"wd": (-5, -4), "xc": (0, 1), "xw": (0.5, 1.5), "nx": (2, 2.5), "ws": (3, 4), "mn": (5, 8), "tail": (6, 9),
          "j": (6.5, 9.5), "end": (7, 10), "u": (11, 12)}
SCAN = [(1, 2, 3)] * 5
MOVED = [8, 4, 8, 4, 8]
XV = [()] * 5
JV = [(), (), ()]
BYDMA = [(0, 1)] * 5
WIDE = ()
XH, XNA = False, True
NLA = True
UW = 1024
SELG = ()


def routes(T, topo, core):
    others = [c for c in T.cores if c != core]
    near = [c for c in others if topo.may_write(core, c)]
    far = [c for c in others if c not in near]
    gates = [c for c in topo.cores_of(core) if c not in T.cores and all(topo.may_write(c, d) for d in far)]
    same = [c for c in gates if topo.die(c) == topo.die(core)]
    other = [c for c in gates if c not in same]
    plan = [{r: far[i::len(rel)] for i, r in enumerate(rel)} for rel in (other[:2], same[:2])]
    spare = [c for c in topo.cores_of(core) if c not in gates and topo.die(c) != topo.die(core)]
    plan[1][spare[0]] = near
    return near, plan


def parts(t):
    x = {"x": ("x", 0, H), "y": ("x", H, H)} if t and XH else {"x": ("x", 0, V)}
    return {**x, "u": ("u", 0, H), "v": ("u", H, H)}


def table(tab, t):
    return "t%s%d" % (tab, t % (3 if tab == "x" else 2))


def bits(engines):
    m = 0
    for e in engines:
        m |= 1 << e
    return m


def dst(topo, d, src):
    rid, pid = topo.addr(d, src)
    return DstId(rid=rid, pnc=pid)


def relay_program(g, core, T, topo, owner):
    q = T.rank_of(owner)
    near, plan = routes(T, topo, owner)
    sent = 0
    for t in range(STEPS):
        for kind, (tab, c0, w) in parts(t).items():
            rel = plan["xu".index(tab)]
            if core not in rel:
                continue
            far = rel[core]
            off = topo.engines(core, far[0])
            sent += len(off)
            g.wait_ge(T.sem[kind + "a%d" % t], len(own_engines(topo, owner, near, core, tab)))
            src = T["t" + tab + "0"][:, t * V + c0:t * V + c0 + w]
            land = T[table(tab, t)][:, q * V + c0:q * V + c0 + w]
            g.remote_dma_fused([RemoteDMATransfer(
                dst_ids=[dst(topo, d, core) for d in far], dma_engine_mask=bits(off),
                remote_sem=T.sem[kind + "a%d" % t], srcs=[src], dsts=[land for d in far])],
                local_sem=T.sem.xl0)
    if sent:
        g.wait_ge(T.sem.xl0, sent)


def own_engines(topo, core, near, relay, tab):
    off = topo.engines(core, near[0]) if tab == "x" else []
    return [e for e in topo.engines(core, relay) if e not in off]


def build(g, core, T, topo, banks):
    q = T.rank_of(core)
    near, plan = routes(T, topo, core)
    ops, tag = [], ["init", -1, 0]

    def op(eng, cost, reads, writes, fn, sem=None, lat=0.0, remote=False, adds=None):
        ops.append({"eng": eng, "cost": cost, "r": reads, "w": writes, "fn": fn, "sem": sem, "lat": lat,
                    "tag": tag[0], "step": tag[1], "half": tag[2], "remote": remote, "adds": adds})

    def R(name, lo=0, n=None):
        return (name, lo, lo + (T[name].shape[1] if n is None else n))

    def B(name):
        return T[banks.get(name, LENT[0]) if name[0] == "~" else name]

    def A(reg):
        return B(reg[0])[:, reg[1]:reg[2]]

    def wid(reg):
        return reg[2] - reg[1]

    def half(reg, h):
        return (reg[0], reg[1] + h * H, reg[1] + h * H + H)

    two = ("sb", "cm", "shm", "trm", "selw", "jd", "tx0", "tx1", "tx2", "zr", "gsel", "gneg", "i16", "off")

    def sc(x):
        return A(x) if isinstance(x, tuple) else x

    def ts(out, in0, s1, op0, s2=None, op1=None):
        fast = out[0] in two and in0[0] in two
        rd = [in0] + [s for s in (s1, s2) if isinstance(s, tuple)]
        if op1 is None:
            fn = lambda: g.vector.tensor_scalar(A(out), A(in0), sc(s1), None, op0)
        else:
            fn = lambda: g.vector.tensor_scalar(A(out), A(in0), sc(s1), sc(s2), op0, op1)
        op("v", FIX + max(64, wid(out) * (0.5 if fast else 1)) * CY, rd, [out], fn)

    def tt(out, in0, in1, alu):
        k = 1 if any(x[0] in PSUM or x[0][0] == "~" for x in (in0, in1)) else 2
        op("v", FIX + max(64, wid(out) * k) * CY, [in0, in1], [out],
           lambda: g.vector.tensor_tensor(A(out), A(in0), A(in1), alu))

    def cp(out, in0):
        op("v", FIX + max(64, wid(out)) * CY, [in0], [out], lambda: g.vector.tensor_copy(A(out), A(in0)))

    def fill(out, x):
        op("v", FIX + max(64, wid(out) * 0.5) * CY, [], [out], lambda: g.vector.memset(A(out), x))

    def act(out, in0, func, bias=0.0, scale=1.0):
        rd = [in0] + [s for s in (bias, scale) if isinstance(s, tuple)]
        op("a", FIX + max(64, wid(out)) * CY, rd, [out],
           lambda: g.scalar.activation(A(out), A(in0), func, bias=sc(bias), scale=sc(scale)))

    def mm(items, reads, writes, adds=None):
        def fn():
            last = None
            for o, l, r, s0, s1, _ in items:
                last = g.tensor.matmul(o, l, r, s0, s1)
            return last
        op("t", 15 + sum(i[5] for i in items) * PE, reads, writes, fn, adds=adds)
        ops[-1]["calls"] = len(items)

    def lin(out, terms, start=True, stop=True):
        n = len(terms)
        mm([(A(out), A(m), A(x), start and i == 0, stop and i == n - 1, wid(x)) for i, (m, x) in enumerate(terms)],
           [m for m, x in terms] + [x for m, x in terms], [out], adds=None if start or stop else (out, tag[1]))

    def dma(eng, out_ap, in_ap, reads, writes, sem, lat=LAT_DMA):
        qq = g.sync if eng == "s" else g.scalar
        op(eng, 60.0, reads, writes, lambda: qq.dma_start(out_ap, in_ap), sem=sem, lat=lat)

    def iota(name, pattern, base, mult):
        n = T[name].shape[1]
        op("g", 130 + 2 * n * CY, [], [R(name)], lambda: g.iota(T[name][:], pattern, base, mult))

    def pick(out, in0, pattern, base, x, mult=1, keep=ALU.not_equal):
        op("g", 170 + 2 * wid(out) * CY, [in0], [out],
           lambda: g.affine_select(A(out), A(in0), pattern, keep, x, base, mult))

    def send(kind, t):
        tab, c0, w = parts(t)[kind]
        own = R(table(tab, t), q * V + c0, w)
        rel = plan["xu".index(tab)]
        off = topo.engines(core, near[0])
        on = own_engines(topo, core, near, list(rel)[0], tab)
        sem = T.sem[kind + "a%d" % t]

        def fn():
            hops = [RemoteDMATransfer(dst_ids=[dst(topo, r, core) for r in rel], dma_engine_mask=bits(on), remote_sem=sem,
                                      srcs=[A(own)], dsts=[T["t" + tab + "0"][:, t * V + c0:t * V + c0 + w] for r in rel])]
            if tab == "x":
                hops.append(RemoteDMATransfer(dst_ids=[dst(topo, d, core) for d in near], dma_engine_mask=bits(off),
                                              remote_sem=sem, srcs=[A(own)], dsts=[A(own) for d in near]))
            g.remote_dma_fused(hops, local_sem=T.sem[kind + "l%d" % t])
            return None
        hold = [R("sentx", 0, 1)] if (kind, t) == ("u", 0) else []
        op("g", 1000.0, [own] + hold, [R("sent" + kind, t, 1), R("turn" + tab, 0, 1)], fn,
           sem=(kind + "l%d" % t, len(on) + (len(off) if tab == "x" else 0)), lat=3000.0, remote=tab)
        op(None, 0.0, [R("sent" + kind, t, 1)], [R("arr" + kind, t, 1)], None,
           sem=(kind + "a%d" % t, len(off) * (len(T.cores) - 1)), lat=(LAT_X if tab == "x" else LAT_U) - 4000.0)

    SB = lambda i: R("sb", i * V, V)
    SF = lambda i: R("sf", i * V, V)
    CM = lambda i: R("cm", i * 128, 128)
    COL = lambda i: R("col", i, 1)
    AG, WW, R1, KEY, FRESH, SS, SW2, XB, WGT, L2 = [SB(i) for i in range(10)]
    NL, CAP, CAP1, ONES, WT = [SB(10), SB(11)], SB(12), SB(13), SB(14), [SB(15), SB(16)]
    JJ0, JJC, CPRE, TMP, OX, OC = [SF(i) for i in range(6)]
    EE, BO, ID, KM, MS, MN, I3, I241, IM15, IM3, IM1, I2, I16TH = [CM(i) for i in range(13)]
    PK, PKH, QF, NB = COL(0), COL(1), COL(2), COL(3)
    TB = lambda d: COL(8 + d - 1)
    DH, DT = R("pd", 0, V), R("pd", V, V)
    OFF = lambda i: R("off", i * V, V)
    XO = lambda t: R(table("x", t), q * V, V)
    UO = lambda t: R(table("u", t), q * V, V)
    ZR = lambda n: R("zr", 0, n)
    HB = lambda h, i: R(("pc", "ph")[h], i * H, H)
    DIAG = [[-1, 128]]

    for i, x in ((4, -241.0), (5, -1.5), (6, -0.5), (7, -39.5), (32, -129.0)):
        fill(COL(i), x)
    fill(R("zr"), 0.0)
    fill(ONES, 1.0)

    dma("s", A(XO(0)), T.x0[:], [], [XO(0)], ("ldx", 16))
    dma("a", A(AG), T.ag[:], [], [AG], ("lda", 16))
    dma("a", A(WW), T.w0[:], [], [WW], ("ldw", 16))
    dma("a", T.si[:], T.s0[:], [], [R("si")], ("lds", 16))
    dma("a", T.cr[:], T.p0[:], [], [R("cr")], ("ldp", 16))
    dma("s", T.jt[:], T.ax[:], [], [R("jt")], ("ldj", 16), lat=LAT_DMA + 1000.0)
    dma("s", A(UO(0)), T.u0[:], [], [UO(0)], ("ldu", 16), lat=LAT_DMA + 1000.0)
    dma("s", T.thi[:], T.th[:], [], [R("thi")], ("ldt", 16), lat=LAT_DMA + 1000.0)
    iota("ia", [[1, 128]], 128, -1)
    iota("ib", [[16, 8], [0, 16]], 143, -1)
    iota("ic", [[1, 144]], -15, -1)
    iota("ip", [[1, 16]], 0, 1)
    for kind in parts(0):
        send(kind, 0)

    ts(R("ia"), R("ia"), 15, ALU.bitwise_and)
    ts(R("ib"), R("ib"), 4, ALU.arith_shift_right)
    ts(R("ib"), R("ib"), 8.0, ALU.not_equal, 16.0, ALU.mult)
    tt(EE, R("ia"), R("ib"), ALU.add)
    ts(BO, EE, 16.0, ALU.is_lt)
    ts(ID, EE, 0.0, ALU.is_equal)
    for m, x in ((I3, 3.0), (I241, 241.0), (IM15, -1.5), (IM3, -3.0), (IM1, -1.0), (I2, 2.0), (I16TH, 1.0 / 16)):
        ts(m, ID, x, ALU.mult)
    for c in range(2 if any(BYDMA) else 0):
        for y in range(2):
            pick(R("bw", (2 * c + y) * 128, 128), ZR(128), [[-32, 4], [256, 2], [-1, 16]], -16 * c - 256 * y, 1.0)
    ts(R("col", 16, 16), R("ia", 0, 16), 0.0, ALU.is_equal)
    for h in range(2):
        if h in SELG:
            pick(R("selw", h * 1024, 1024), ZR(1024), [[-2, 8], [-16, 8], [0, 16]], -h, 1.0)
        else:
            for i in range(8):
                act(R("selw", h * 1024 + i * 128, 128), BO, ACT.Copy, scale=COL(16 + 2 * i + h))
        pick(R("jd", h * 1024, 1024), ZR(1024), [[-256, 8], [-16, 8], [255, 16]], -2048 * h, 8.0)
    pick(R("seg"), ZR(1024), [[0, 64], [1, 16]], 0, 1.0, mult=0, keep=ALU.is_equal)
    ts(R("ip"), R("ip"), 15, ALU.bitwise_and)
    cp(PK, R("ip", 0, 1))
    ts(PKH, PK, 0.5, ALU.mult)
    ts(R("col", 8, 8), R("ip", 1, 8), PK, ALU.is_lt, -0.5, ALU.add)
    ts(R("gsel"), R("ic"), PK, ALU.add, 0.0, ALU.is_equal)
    ts(R("gneg"), R("gsel"), -1.0, ALU.mult)
    ts(R("i16"), ID, 2.0 ** -8, ALU.mult)
    ts(R("i32", 0, 128), ID, 2.0 ** -11, ALU.mult)
    ts(R("i32", 128, 128), ID, 0.5, ALU.mult)
    for name, ds in (("shm", range(15, 7, -1)), ("trm", range(1, 8))):
        for i, d in enumerate(ds):
            ts(R(name, i * 128, 128), EE, float(d), ALU.is_equal)
        m = R(name, 0, 128 * len(ds))
        pick(m, m, [[0, len(ds)]] + DIAG, 0, -1.0)
    ts(KM, R("ia"), 0.0, ALU.is_equal)
    pick(MS, KM, DIAG, 0, 33.0)
    ts(MN, BO, 2.0, ALU.mult)
    pick(MN, MN, DIAG, 0, -62.0)
    BOM = {16: BO}
    for m in sorted(set(MOVED) - {0, 16}):
        BOM[m] = CM(12 + len(BOM))
        pick(BOM[m], BO, [[0, 32], [1, 4]], m // 4 - 4, 0.0, mult=0, keep=ALU.is_ge)
    ts(QF, R("thi", 0, 1), -1.0, ALU.mult, 0.5, ALU.add)
    ts(NB, R("thi", 1, 1), -1.0, ALU.mult, 0.5, ALU.add)
    lent = [0]

    def bank():
        lent[0] += 1
        return "~%d" % lent[0]

    def weights(t, h):
        lin(HB(h, 1), [(ID, half(R1, h)), (I3, half(NL[t % 2], h)), (ID, half(ONES, h))])
        tt(half(WGT, h), half(WW, h), HB(h, 1), ALU.mult)

    def spread(t, h):
        if h not in BYDMA[t]:
            return
        tag[0], tag[2] = "wd", h
        d, wd, ws = R(bank(), 0, H), "wd%d%d" % (t % 2, h), R("ws%d" % (t % 2), h * 2048, 2048)
        w, wa, wb = half(WGT, h), half(WT[0], h), half(WT[1], h)
        mm([(B(d[0])[:, 32 * b + 16 * c:32 * b + 16 * c + 16], T.bw[:, (2 * c + y) * 128:(2 * c + y + 1) * 128],
             T.sb[:, w[1] + 2 * b + y:w[2]:8], y == 0, y == 1, 64) for b in range(4) for c in range(2) for y in range(2)],
           [w, R("bw")], [d])
        act(wa, d, ACT.Copy)
        op("v", FIX + 64 * CY, [wa], [wb], lambda: g.vector.transpose(A(wb), A(wa)))
        for i in range(2):
            dma("s", T[wd][:, i, :], A(wb), [wb], [R(wd, i, 1)], ("wd%d%d" % (t, h), 16), lat=LAT_T)
        for i in range(8):
            dma("s", T[ws[0]][i:128:8, ws[1]:ws[2]], T[wd][:], [R(wd)], [ws], ("wi%d%d" % (t, h), 16), lat=LAT_W)
            ops[-1]["adds"] = ("ws", t, h)

    def gather(eng, out, tab, offs, c, extra):
        o = R("off", offs * V + c * 64, 64)
        if eng == "a":
            fn = lambda: g.scalar.activation(A(out), T[tab][:, 0:WIN].indirect(A(o)), ACT.Copy)
        else:
            fn = lambda: g.vector.tensor_copy(A(out), T[tab][:, 0:WIN].indirect(A(o)))
        op(eng, FIX + 1024 * GA * CY, [R(tab), o] + extra, [out], fn)
        ops[-1]["ga"] = 1024

    def jumps(offs, out, on_vector, h):
        for c in (2 * h, 2 * h + 1):
            gather("v" if c in on_vector else "a", R("jg", c * 1024, 1024), "jt", offs, c, [])
        b, o = h * 2048, R(bank(), 0, H)
        mm([(A(o), T.jd[:, k * 128:(k + 1) * 128], T.jg[:, b + k:b + 2048:16], k == 0, k == 15, H) for k in range(16)],
           [R("jd"), R("jg", b, 2048)], [o])
        act(half(out, h), o, ACT.Identity, bias=PKH)

    def select(mask, val, h):
        dh, dt, tmp = half(DH, h), half(DT, h), half(TMP, h)
        tt(dt, half(val, h), dh, ALU.subtract)
        tt(tmp, dt, half(mask, h), ALU.mult)
        tt(dh, dh, tmp, ALU.add)

    ts(R1, AG, -1.0, ALU.mult, 3.0, ALU.add)
    ts(NL[0], AG, 3.0, ALU.is_ge)
    for h in range(2):
        weights(0, h)
    tag[0] = "init"
    cp(OFF(STEPS), R("si"))
    tt(DT, R("si"), R("cr"), ALU.subtract)
    tt(TMP, DT, NL[0], ALU.mult)
    ts(DH, DT, 0.5, ALU.mult)
    tt(R("ci"), TMP, R("cr"), ALU.add)
    cp(OFF(0), R("ci"))
    for h in range(2):
        tag[0], tag[2] = "j", h
        jumps(STEPS, JJ0, JV[0], h)

    def activity(t, h):
        tx, ws, hb = table("x", t), "ws%d" % (t % 2), bank()
        tag[2] = h
        tag[0] = "xc"
        for c in (2 * h, 2 * h + 1):
            gather("v" if c in XV[t] else "a", R("xc", c * 1024, 1024), tx, t, c, [R("arrx", t, 1), R("arry", t, 1)])
        n = 128 if h in WIDE else 64
        s, m = n // 32, 512 // n
        for v0 in range(h * H, h * H + H, n):
            c0 = 16 * v0
            for e in range(s):
                b, o = bank(), R("wx", c0 + e * 512, 512)
                tag[0] = "xw"
                sel = [R("selw", (k % 2 * 8 + k // 2) * 128, 128) for k in range(e, 16, s)]
                mm([(B(b)[:, i:512:m], A(sel[i]), T.sb[:, WGT[1] + v0:WGT[1] + v0 + n], True, True, n) for i in range(m)],
                   sel + [half(WGT, h)], [R(b, 0, 512)])
                op("v", FIX + 512 * CY, [R("xc", c0, 16 * n), R(b, 0, 512)], [o],
                   lambda o=o, b=b, c0=c0, e=e: g.vector.tensor_tensor(A(o), T.xc[:, c0 + e:c0 + 16 * n:s], B(b)[:], ALU.mult))
                if h not in BYDMA[t]:
                    tag[0] = "ws"
                    op("a", FIX + 512 * CY, [R(b, 0, 512)], [R(ws, c0, 16 * n)],
                       lambda b=b, c0=c0, e=e: g.scalar.activation(T[ws][:, c0 + e:c0 + 16 * n:s], B(b)[:], ACT.Copy),
                       adds=("ws", t, v0))
            tag[0] = "xw"
            o = R(hb, v0 - h * H, n)
            for k0 in range(0, 16, 1024 // n):
                mm([(A(o), T.i16[:], T.wx[:, c0 + k // m * 512 + k % m:c0 + k // m * 512 + 512:m], k == 0, k == 15, n)
                    for k in range(k0, k0 + 1024 // n)], [R("i16"), R("wx", c0 + k0 * n, 1024)], [o])
        tag[0] = "nx"
        xn, e = half(XO(t + 1), h), R(bank(), 0, H)
        ts(half(XB, h), R(hb, 0, H), 15.0, ALU.min, 128.501953125, ALU.add)
        if XNA:
            act(xn, half(XB, h), ACT.Identity, bias=COL(32))
        else:
            ts(xn, half(XB, h), -129.0, ALU.add)
        lin(e, [(BO, xn)])
        act(half(SS, h), e, ACT.Sign, bias=NB)
        if t == STEPS - 1:
            act(half(OX, h), xn, ACT.Copy)
            dma("s", T.yx[:, h * H:h * H + H], A(half(OX, h)), [half(OX, h)], [], ("out", 16))

    def tags(t, h):
        last, mv, c0 = t == STEPS - 1, MOVED[t], h * 2048
        x, nl, dt, dh = half(XO(t), h), half(NL[t % 2], h), half(DT, h), half(DH, h)
        key, fresh, cap, r1, ww = [half(y, h) for y in (KEY, FRESH, CAP, R1, WW)]
        ci, cr = half(R("ci"), h), half(R("cr"), h)
        C, Z = HB(h, 0), HB(h, 1)
        tag[0], tag[2] = "mn", h
        lin(C, [(I241, nl)], stop=False)
        if mv < 16:
            x4 = R(bank(), 0, 512)
            mm([(B(x4[0])[:, i:512:4], A(ID), A(x), True, True, H) for i in range(4)], [ID, x], [x4])
        for j in range(4):
            o = R("mn", c0 + j * 512, 512)
            if j < 4 - mv // 4:
                op("v", FIX + 512 * CY, [R("xc", c0, 2048), x4], [o],
                   lambda j=j, o=o: g.vector.tensor_tensor(A(o), T.xc[:, c0 + j:c0 + 2048:4], A(x4), ALU.min))
                sign = "gsel"
            else:
                b, sign = bank(), "gneg"
                mm([(B(b)[:], A(IM1), T.xc[:, c0 + j:c0 + 2048:4], True, False, 512)]
                   + [(B(b)[:, i:512:4], A(ID), A(x), False, i == 3, H) for i in range(4)],
                   [ID, IM1, x, R("xc", c0, 2048)], [R(b, 0, 512)])
                act(o, R(b, 0, 512), ACT.Relu)
            end = j == 3 and not mv
            mm([(A(C), T[sign][:, 15 - j - 4 * i:143 - j - 4 * i], T.mn[:, o[1] + i:o[2]:4], False, end and i == 3, H)
                for i in range(4)], [R(sign), o], [C], adds=None if end else (C, t))
        if mv:
            lin(C, [(BOM[mv], x)], start=False)
        tag[0] = "tail"
        act(key, C, ACT.Identity, bias=COL(4))
        act(fresh, key, ACT.Sign, bias=QF)
        lin(Z, [(MN, nl)], stop=False)
        sg = lambda d: R("sg", h * 1024 + (d - 1) * H, H)
        for d4 in range(2):
            b, ds = bank(), range(4 * d4 + 1, 4 * d4 + 5)
            mm([(B(b)[:, (d - ds[0]) * H:(d - ds[0] + 1) * H], T.shm[:, (d - 1) * 128:d * 128], A(key), True, True, H)
                for d in ds], [R("shm"), key], [R(b, 0, 512)])
            for d in ds:
                act(sg(d), R(b, (d - ds[0]) * H, H), ACT.Sign, bias=TB(d))
            for d in ds[::2]:
                lin(Z, [(R("trm", (j - 1) * 128, 128) if j < 8 else IM1, sg(j)) for j in (d, d + 1)], start=False, stop=False)
        lin(Z, [(MS, half(SS, h))], start=False)
        act(cap, Z, ACT.Sign, bias=COL(7))
        tag[0] = "j"
        if t == 0:
            select(NL[0], JJ0, h)
        if t in (1, 3):
            act(half(CAP1, h), cap, ACT.Relu)
            jumps(t, JJC, JV[(t + 1) // 2], h)
            select(NL[t % 2], JJC, h)
        if t == 1:
            ts(half(L2, h), r1, 1.0, ALU.is_equal)
        if t == 2:
            select(L2, JJ0, h)
        if t in (2, 4):
            select(CAP1, JJC, h)
        tag[0] = "end"
        tt(half(CPRE, h), ci, dh, ALU.add)
        lin(HB(h, 2), [(IM1, r1), (IM3, nl), (ID, fresh), (IM1, cap)])
        act(half(SW2, h), HB(h, 2), ACT.Sign, bias=COL(5), scale=-1.0)
        tt(dh, dh, half(SW2, h), ALU.mult)
        tt(cr, half(CPRE, h), dh, ALU.subtract)
        ts(ci, cr, WIN - 1, ALU.bitwise_and)
        if not last:
            cp(half(OFF(t + 1), h), ci)
        else:
            cp(half(OC, h), ci)
            dma("s", T.yc[:, h * H:h * H + H], A(half(OC, h)), [half(OC, h)], [], ("out", 16))
        lin(HB(h, 3), [(ID, r1), (I2, fresh), (IM15, cap)])
        act(r1, HB(h, 3), ACT.Relu, bias=COL(6))
        lin(C, [(ID, ww), (I2, cap)])
        ts(ww, C, 2.0, ALU.add, 15.0, ALU.min)
        if not last:
            if NLA:
                act(half(NL[1 - t % 2], h), r1, ACT.Relu, bias=R("sb", ONES[1], 1), scale=-1.0)
            else:
                ts(half(NL[1 - t % 2], h), r1, 1.0, ALU.is_lt)
            weights(t + 1, h)
        else:
            ts(dt, r1, -16.0, ALU.mult, 48.0, ALU.add)
            tt(half(JJ0, h), dt, ww, ALU.add)
            dma("s", T.yw[:, h * H:h * H + H], A(half(JJ0, h)), [half(JJ0, h)], [], ("out", 16))

    def potentials(t):
        tx, tu, ws = table("x", t), table("u", t), "ws%d" % (t % 2)
        tag[0] = "u"
        for c in range(4):
            v0, b0, s0 = c * 64, c * 1024, (c % 2) * 1024
            tag[2] = c // 2
            for b1 in range(b0, b0 + 1024, UW):
                o = R("off", t * V + b1 // 16, UW // 16)
                op("v", FIX + UW * GA * CY, [R(tu), o, R(ws, b0, 1024), R("arru", t, 1), R("arrv", t, 1)], [R("wu", b1, UW)],
                   lambda o=o, b1=b1: g.vector.tensor_tensor(
                       T.wu[:, b1:b1 + UW], T[tu][:, 0:WIN].indirect(A(o)), T[ws][:, b1:b1 + UW], ALU.mult))
                ops[-1]["ga"] = UW
            r, x, u = R("pr", v0, 64), R(tx, q * V + v0, 64), R(tu, q * V + v0, 64)
            items = ([(A(r), A(I16TH), A(x), True, False, 64), (A(r), T.i32[:, 128:256], A(u), False, False, 256)]
                     + [(A(r), T.i32[:, 0:128], T.wu[:, b0 + k:b0 + 1024:16], False, k == 15, 256) for k in range(16)])
            if c in SCAN[t]:
                op("v", FIX + 1024 * CY, [R("seg"), R("wu", b0, 1024)], [R("su", s0, 1024)],
                   lambda b0=b0, s0=s0: g.vector.tensor_tensor_scan(
                       T.su[:, s0:s0 + 1024], T.seg[:], T.wu[:, b0:b0 + 1024], 0.0, ALU.mult, ALU.add))
                mm(items[:2] + [(A(r), T.i32[:, 0:128], T.su[:, s0 + 15:s0 + 1024:16], False, True, 256)],
                   [I16TH, R("i32"), x, u, R("su", s0, 1024)], [r])
            for i in range(0, 0 if c in SCAN[t] else 18, 2):
                mm(items[i:i + 2], [I16TH, R("i32"), x, u, R("wu", b0, 1024)], [r])
            if c % 2:
                un = half(UO(t + 1), c // 2)
                act(un, R("pr", v0 - 64, H), ACT.Tanh, bias=COL(6))
                if t < STEPS - 1:
                    send("uv"[c // 2], t + 1)
                else:
                    dma("s", T.yu[:, v0 - 64:v0 + 64], A(un), [un], [], ("out", 16))

    for t in range(STEPS):
        tag[1] = t
        for h in range(2):
            spread(t, h)
            activity(t, h)
            if t < STEPS - 1 and (XH or h):
                send("xy"[h] if XH else "x", t + 1)
        tags(t, 0)
        tags(t, 1)
        potentials(t)
    return ops


def in_turn(a, b):
    return a["eng"] == b["eng"] == "t" or (a["remote"] and a["remote"] == b["remote"])


def meet(a, b):
    return a[0] == b[0] and a[1] < b[2] and b[1] < a[2]


def depend(ops):
    n = len(ops)
    deps = [set() for _ in range(n)]
    seen = {}
    for i, o in enumerate(ops):
        for reg, wr in [(x, False) for x in o["r"]] + [(x, True) for x in o["w"]]:
            bank = wr and o["eng"] == "t" and reg[0] in ("pc", "ph", "pr")
            for j, reg2, wr2 in seen.get(reg[0], []):
                if j != i and ((wr or wr2) and meet(reg, reg2) or bank and wr2):
                    if not (o["adds"] and o["adds"] == ops[j]["adds"]):
                        deps[i].add(j)
        for reg, wr in [(x, False) for x in o["r"]] + [(x, True) for x in o["w"]]:
            seen.setdefault(reg[0], []).append((i, reg, wr))
    return deps


def lay(ops, pred, succ, uses, rank, first, before):
    n = len(ops)
    left = [len(d) for d in pred]
    at, end, ready = [0.0] * n, [0.0] * n, {}
    free, touched, banks, order = {e: 0.0 for e in ("v", "a", "t", "g", "s", None)}, {}, {}, []
    holder = {b: None for b in LENT}
    todo = {x: len(uses[x]) for x in uses}
    back = {b: -SYNC for b in LENT}
    eng = [o["eng"] for o in ops]
    cost = [o["cost"] for o in ops]
    for i in range(n):
        if not left[i]:
            ready[i] = first[i]
    done = [False] * n
    while ready:
        c, who, est = 1e18, None, {}
        idle = [back[x] for x in LENT if holder[x] is None]
        for i, s in ready.items():
            e = eng[i]
            if free[e] > s:
                s = free[e]
            for b in ops[i]["banks"]:
                if b in touched:
                    for f, x in touched[b].items():
                        if f != e and x + SYNC > s:
                            s = x + SYNC
                elif b[0] == "~":
                    if not idle or not all(done[j] for j, x in before[b]):
                        s = None
                        break
                    s = max([s, min(idle) + SYNC] + [end[j] + x - cost[i] - EARLY for j, x in before[b]])
            if s is not None:
                est[i] = s
                if s + cost[i] < c:
                    c, who = s + cost[i], i
        if who is None:
            return None
        i, e = who, eng[who]
        if e:
            i = min((j for j in est if eng[j] == e and est[j] < c), key=lambda j: rank[j] + HASTE * est[j])
        s = est[i]
        at[i], end[i] = s, s + cost[i]
        done[i] = True
        if e:
            free[e] = end[i]
        for b in ops[i]["banks"]:
            if b[0] == "~":
                if b not in banks:
                    x = max((x for x in LENT if holder[x] is None and back[x] + SYNC <= s + 1e-6), key=lambda x: back[x])
                    banks[b], holder[x] = x, b
                todo[b] -= 1
                back[banks[b]] = max(back[banks[b]], end[i])
                if not todo[b]:
                    holder[banks[b]] = None
            touched.setdefault(b, {})[e] = end[i]
        order.append(i)
        del ready[i]
        for j, x in succ[i]:
            left[j] -= 1
            if not left[j]:
                ready[j] = max([first[j]] + [end[k] + y for k, y in pred[j]])
    return order, banks, at, end


def schedule(ops, seed):
    n = len(ops)
    deps = depend(ops)
    uses, pred, succ = {}, [[] for _ in range(n)], [[] for _ in range(n)]
    for i in range(n):
        ops[i]["banks"] = sorted(set(x[0] for x in ops[i]["r"] + ops[i]["w"] if x[0] in PSUM or x[0][0] == "~"))
        for b in ops[i]["banks"]:
            if b[0] == "~":
                uses.setdefault(b, []).append(i)
        e = ops[i]["eng"]
        for j in sorted(deps[i]):
            f = ops[j]["eng"]
            x = (SYNC if f != e else 0.0 if e == "t" else 60.0) + (0.0 if in_turn(ops[i], ops[j]) else ops[j]["lat"])
            pred[i].append((j, x))
            succ[j].append((i, x))
    on = {}
    for i, o in enumerate(ops):
        on.setdefault((o["eng"], o["tag"], o["step"], o["half"]), []).append(i)
    for t in range(STEPS):
        for e, first, then, dt in FENCES:
            for a in [i for x in first.split() for i in on.get((e, x[:-1], t, int(x[-1])), [])]:
                for b in [i for x in then.split() for i in on.get((e, x[:-1], t + dt, int(x[-1])), [])]:
                    pred[b].append((a, 0.0))
                    succ[a].append((b, 0.0))
    left = [len(x) for x in pred]
    turn = [i for i in range(n) if not left[i]]
    for i in turn:
        for j, x in succ[i]:
            left[j] -= 1
            if not left[j]:
                turn.append(j)
    fore, aft, safe = {}, {}, {}
    for b in uses:
        reader = [i for i in uses[b] if ops[i]["eng"] != "t"][0]
        fore[b] = [(j, x) for j, x in pred[reader] if j not in uses[b]]
        safe[b] = fore[b] + [(j, -1e9) for i in uses[b] for j, x in pred[i] if j not in uses[b]]
        aft[b] = [(j, -1e9) for i in uses[b] for j, x in succ[i] if j not in uses[b]]
    lat, zero, level = [o["lat"] for o in ops], [0.0] * n, [0.0] * n
    kind = [(o["tag"], o["step"], o["half"]) for o in ops]
    for i in reversed(turn):
        level[i] = ops[i]["cost"] + max([lat[i]] + [level[j] + x for j, x in succ[i]])
    top, kinds, state = {}, sorted(set(kind)), [seed]
    for i in range(n):
        top[kind[i]] = max(top.get(kind[i], 0.0), level[i])

    def chance():
        state[0] = (state[0] * 1103515245 + 12345) % 2147483648
        return (state[0] >> 8) / 8388608.0

    def span(got):
        order, banks = got[0], got[1]
        end, free, used = [0.0] * n, {}, {}
        for i in order:
            e = ops[i]["eng"]
            s = max([free.get(e, 0.0)] + [end[j] + x + late[j] for j, x in pred[i]])
            for b in ops[i]["banks"]:
                for f, x in used.setdefault(banks.get(b, b), {}).items():
                    if f != e and x + SYNC > s:
                        s = x + SYNC
            end[i] = s + ops[i]["cost"] * (SLOW if e == "t" else 1.0)
            for b in ops[i]["banks"]:
                used[banks.get(b, b)][e] = end[i]
            if e:
                free[e] = end[i]
        return max(got[3][i] + lat[i] for i in range(n)) + CARE * max(end)
    late = [LATE if o["eng"] is None else 0.5 * o["lat"] if o["eng"] == "s" else 0.0 for o in ops]
    rank = [-1e5 - level[i] if kind[i][0] == "init" else
            1000.0 * (PERIOD * max(0, kind[i][1]) + PHASES[kind[i][0]][kind[i][2]]) + 0.1 * (top[kind[i]] - level[i])
            for i in range(n)]
    now = lay(ops, pred, succ, uses, rank, zero, safe)
    best = now = now + (span(now),)
    for turn in range(TURNS):
        shift = {kinds[int(chance() * len(kinds))]: (2 * chance() - 1) * JITTER for _ in range(1 + int(6 * chance()))}
        rank = [shift.get(kind[i], 0.0) - now[3][i] for i in range(n)]
        got = lay(ops, succ, pred, uses, rank, lat, {b: [] for b in uses}) or lay(ops, succ, pred, uses, rank, lat, aft)
        rank = [-got[3][i] - URGE * lat[i] - RUSH.get(kind[i][::2], 0.0) for i in range(n)]
        got = lay(ops, pred, succ, uses, rank, zero, fore) or lay(ops, pred, succ, uses, rank, zero, safe)
        got += (span(got),)
        if got[4] <= now[4] + DRIFT * chance():
            now = got
            if now[4] < best[4]:
                best = now
    order, banks = best[0], best[1]
    used = {}
    for i in order:
        e = ops[i]["eng"]
        for b in ops[i]["banks"]:
            b = banks.get(b, b)
            deps[i].update(j for e2, j in used.get(b, {}).items() if e2 != e)
            used.setdefault(b, {})[e] = i
    return order, deps, banks


PLAN = {}


def rank_program(g, core, T, topo):
    if T.rank_of(core) is None:
        for owner in topo.cores_of(core):
            if T.rank_of(owner) is not None:
                relay_program(g, core, T, topo, owner)
        return
    if "order" not in PLAN:
        PLAN["order"], PLAN["deps"], PLAN["banks"] = schedule(build(g, core, T, topo, {}), SEED)
    order, deps = PLAN["order"], PLAN["deps"]
    ops = build(g, core, T, topo, PLAN["banks"])
    queue = {"v": g.vector, "a": g.scalar, "t": g.tensor, "g": g, "s": g.sync}
    needed = set(j for i in order for j in deps[i] if ops[i]["eng"] is not None and not in_turn(ops[i], ops[j]))
    token, waited, total = {}, {}, {}
    for i in order:
        o = ops[i]
        e = o["eng"]
        if e is not None:
            want = {}
            for j in deps[i]:
                if j in token and not in_turn(o, ops[j]):
                    s, x = token[j]
                    want[s] = max(want.get(s, 0), x)
            for s in sorted(want):
                if waited.get((e, s), 0) < want[s]:
                    queue[e].wait_ge(T.sem[s], want[s])
                    waited[(e, s)] = want[s]
        ins = o["fn"]() if o["fn"] else None
        if o["sem"]:
            s, x = o["sem"]
            if ins is not None:
                ins.then_inc(T.sem[s], x)
            total[s] = total.get(s, 0) + x
            token[i] = (s, total[s])
        elif i in needed:
            s = "q" + e
            ins.then_inc(T.sem[s], 1)
            total[s] = total.get(s, 0) + 1
            token[i] = (s, total[s])
    for s in sorted(total):
        if not any(waited.get((e, s), 0) >= total[s] for e in queue):
            g.wait_ge(T.sem[s], total[s])
